import numpy as np, ml_dtypes
CORES = [16,17,18,19,32,33,34,35]
N = 8
import mx_ref
BF = ml_dtypes.bfloat16
def gentries(a):
    return np.ascontiguousarray(a.reshape(8, 16, -1).transpose(0, 2, 1)).reshape(8, -1)
def gtable(e):
    e = np.asarray(e); return np.ascontiguousarray(e.reshape(8, -1, 16).transpose(0, 2, 1)).reshape(128, -1).astype(np.int32)
def gcols(t, e):
    v = np.concatenate([t.reshape(8, 16, -1, 4), np.zeros((8, 16, 1, 4), BF)], axis=2)
    return np.ascontiguousarray(np.stack([v[g][:, e[g]] for g in range(8)])).reshape(128, -1)
def tile(rs):
    return np.stack(rs, axis=2).reshape(128, -1).astype(BF)
def cut(t, i, w=512):
    return t[:, w * i:w * i + w]
def pick(q, e):
    c = np.concatenate([q[0].reshape(128, -1, 4), np.zeros((128, 1, 4), np.uint8)], axis=1); s = np.concatenate([q[1], np.ones((16, 1), np.uint8)], axis=1)
    return (np.ascontiguousarray(c[:, e].reshape(128, -1)), np.ascontiguousarray(s[:, e]))
def join(*qs):
    return (np.concatenate([q[0] for q in qs], axis=1), np.concatenate([q[1] for q in qs], axis=1))
def put(q, e, v):
    c, s = q[0].reshape(128, -1, 4).copy(), q[1].copy(); c[:, e] = v[0].reshape(128, -1, 4); s[:, e] = v[1]
    return (c.reshape(128, -1), s)
def pk(c, s):
    return (np.ascontiguousarray(c), mx_ref.live(s))
def emit(q):
    return q[0], q[1]
def packed(v, rng):
    q = [mx_ref.quantize(np.ascontiguousarray(v[r])) for r in range(N)]
    return np.stack([a for a, b in q]), np.stack([mx_ref.plane(b, rng) for a, b in q])
def values_of_codes():
    e, c = np.zeros((128, 128, 4), np.float32), np.zeros((128, 2, 4), np.uint8)
    e[np.arange(128), np.arange(128), 0] = 1
    c[:127, :, 0] = np.arange(256).reshape(2, 128).T[:127]
    return mx_ref.matmul(mx_ref.quantize(e.reshape(128, 512).astype(BF)), (c.reshape(128, 8), np.full((16, 2), 127, np.uint8))).T.reshape(-1).astype(np.float64)
CODE_VALUE, SCALE_VALUE = values_of_codes(), 2.0 ** (np.arange(256) - 127.0)
def decode(q):
    return (CODE_VALUE[q[0]].reshape(16, 8, -1, 4) * SCALE_VALUE[q[1]][:, None, :, None] + 0.0).reshape(128, -1).astype(np.float32)
def f(rng, *shape):
    return mx_ref.flush((rng.standard_normal(shape, dtype=np.float32) * np.exp2(rng.integers(-2, 3, shape[:-1] + (1,)))).astype(BF))
def wide(rng, *shape, cols=0):
    v = rng.standard_normal(shape, dtype=np.float32) * np.exp2(rng.integers(-12, 13, shape)).astype(np.float32)
    if cols: v *= np.repeat(np.exp2(rng.integers(-cols, cols + 1, shape[:-2] + (1, shape[-1] // 4))) * (rng.random(shape[:-2] + (1, shape[-1] // 4)) > 0.0625), 4, axis=-1).astype(np.float32)
    return mx_ref.flush(v.astype(BF))
C, G, R, L = 448, 256, 3, 3
def big(v, k):
    v = v.astype(np.float32) * np.float32(k)
    v[np.abs(v) < np.float32(2.0 ** -16)] = 0
    return v.astype(BF)
def numbers_of(rng):
    return {"x": big(f(rng, N, 128, 4 * C), 1), "gh": big(f(rng, N, 128, 4 * G), 1), "u": np.array(f(rng, N, 128, 512)), "v": np.array(f(rng, N, 128, 512))}
def weights(rng, w):
    c, p = packed(np.stack([w] * N), rng)
    return {"wc": c, "ws": p}
def still(rng):
    w = np.zeros((128, 4, 128, 4), np.float32)
    i = np.arange(128)
    for b in range(4): w[i, b, i, b] = 32
    return weights(rng, w.reshape(128, 2048).astype(BF))
def matching(rng, n):
    p, i = np.arange(C), rng.permutation(C)[:n]
    h = n // 2
    p[i[:h]] = i[h:2 * h]
    p[i[h:2 * h]] = i[:h]
    return p
def stored(nx, pr):
    return {"nx": np.stack([gtable(nx[r]) for r in range(N)]), "pr": np.stack([gtable(pr[r].reshape(8, R * C)) for r in range(N)])}
def lists_of(rng, same=(), halves=()):
    nx = rng.permuted(np.tile(np.arange(C + G), (N, 8, 1)), axis=2)
    for r in same: nx[r] = nx[r, 0].copy()
    pr = np.stack([matching(rng, C) for i in range(N * 8 * R)]).reshape(N, 8, R, C)
    h = C // 2
    for r in halves:
        for g in range(8):
            for lo, hi in ((0, h), (h, C), (C, C + G)): nx[r, g, lo:hi] = lo + rng.permutation(hi - lo)
            i = h + rng.permutation(h)
            pr[r, g, 0, :h] = i
            pr[r, g, 0, i] = np.arange(h)
    return stored(nx, pr)
def signs(rng):
    return np.stack([rng.permutation(8) % 2 * 2.0 - 1.0 for r in range(N)])
def linked(rng, kind):
    i, a, b, n = rng.permutation(C + G), rng.permutation(C), C + rng.permutation(G), np.arange(C + G)
    if kind == 1: n[i] = np.roll(i, -1)
    if kind == 2:
        n[a] = np.roll(a, -1)
        n[b] = np.roll(b, -1)
    if kind == 3:
        i = np.concatenate([np.stack([a[:G], b], axis=1).reshape(-1), a[G:]])
        n[i] = np.roll(i, -1)
    if kind == 4:
        n[i[::2]] = i[1::2]
        n[i[1::2]] = i[::2]
    if kind == 5: n = np.roll(n, -1)
    if kind == 6: n = np.roll(n, 1)
    if kind == 7: n = i
    return n
def setup_inputs(rng):
    return {**numbers_of(rng), **lists_of(rng), **weights(rng, f(rng, 128, 2048))}
def setup_inputs_ties(rng):
    d = numbers_of(rng)
    c = big(f(rng, 128, 4), 1).astype(np.float32).reshape(8, 16, 4)[:, :8]
    k = np.stack([rng.permutation(C + G) % 2 for r in range(N)])
    k[rng.integers(N)] = 1
    a = np.where(k[:, None, None, :, None] == 1, c[None, :, :, None, :], np.float32(0.0)).astype(BF)
    d["x"].reshape(N, 8, 16, C, 4)[:, :, :8] = a[:, :, :, :C]
    d["gh"].reshape(N, 8, 16, G, 4)[:, :, :8] = a[:, :, :, C:]
    keep = np.zeros((8, 16, 8), bool)
    for g in range(8): keep[g, :8, g] = True
    u = d["u"].reshape(N, 8, 16, 128, 4)
    a = u[:, :, :, ::16].astype(np.float32)
    a[:, ~keep] = 0
    u[:, :, :, ::16] = a.astype(BF)
    w = np.array(f(rng, 128, 2048)).reshape(8, 16, 4, 8, 16, 4)
    w[:, 8:, :, :, :8] = 0
    for g in range(8):
        for h in range(8):
            if g != h: w[h, :, :, g, :8] = 0
    return {**d, **lists_of(rng), **weights(rng, w.reshape(128, 2048))}
def setup_inputs_near(rng):
    d = numbers_of(rng)
    m = np.stack([rng.permutation(8) + 1 for r in range(N)])
    s = rng.integers(0, 2 ** m[:, :, None], (N, 8, C + G))
    sg, o = signs(rng), rng.permutation(N)
    full = int(np.flatnonzero(o == 3)[0])
    h = 2 ** (m[full][:, None] - 1)
    s[full] = s[full] % h + h * ((np.arange(C + G) >= C // 2)[None, :] == (sg[full] > 0)[:, None])
    g = ((s[..., None] >> np.arange(8)) & 1) * np.exp2(np.arange(8) - 23.0)
    a = np.abs(np.concatenate([d["x"], d["gh"]], axis=2).astype(np.float32)).reshape(N, 8, 16, C + G, 4)
    a[:, :, 0] = 0
    a[:, :, 0, :, 0] = 0.5
    a[:, :, 8] = g[..., :4]
    a[:, :, 9] = g[..., 4:]
    a[:, :, 10:] = rng.integers(4, 8, (N, 8, 6, C + G, 4)) * 2.0 ** -20
    a = (a * np.float32(2.0 ** -7)).reshape(N, 128, 4 * (C + G)).astype(BF)
    k = sg * np.exp2(np.array([-30.0, 0.0, 24.0])[o % 3])[:, None]
    u = d["u"].reshape(N, 128, 128, 4)
    u[:, :, ::16] = 0
    for h in range(8):
        z = k[:, h].astype(np.float32).astype(BF)
        u[:, 16 * h, 16 * h, 0] = z
        u[:, 16 * h + 8:16 * h + 10, 16 * h] = z[:, None, None]
    return {**d, "x": np.ascontiguousarray(a[:, :, :4 * C]), "gh": np.ascontiguousarray(a[:, :, 4 * C:]), **lists_of(rng, (), (full,)), **still(rng)}
def setup_inputs_huge(rng):
    d = numbers_of(rng)
    a = 2.0 ** 29 * (0.6 + 0.4 * rng.random((N, 128, C + G, 4)))
    c = np.stack([rng.permutation(C + G) % 2 * 2.0 - 1.0 for r in range(N)])
    one = rng.permutation(N) < N // 2
    c[one] = 1
    a = (a * c[:, None, :, None]).astype(np.float32).reshape(N, 128, 4 * (C + G)).astype(BF)
    z = 2.0 ** 30 * (1 - 0.25 * rng.random((N, 128, 8, 4))) * signs(rng)[:, None, :, None]
    d["u"].reshape(N, 128, 128, 4)[:, :, ::16] = z.astype(np.float32).astype(BF)
    return {**d, "x": np.ascontiguousarray(a[:, :, :4 * C]), "gh": np.ascontiguousarray(a[:, :, 4 * C:]), **lists_of(rng, np.flatnonzero(~one)), **still(rng)}
def setup_inputs_shapes(rng):
    e = rng.permutation(N)
    kinds = np.stack([rng.permutation(8) for r in range(N)])
    kinds[e[0]] = 2
    kinds[e[1]] = 3
    nx = np.stack([linked(rng, kinds[r, g]) for r in range(N) for g in range(8)]).reshape(N, 8, C + G)
    j = np.arange(C)
    pr = np.zeros((N, 8, R, C), int)
    for r in range(N):
        o = rng.permutation(8)
        for g in range(8):
            for t in range(R): pr[r, g, t] = (j, j ^ 1, C - 1 - j, matching(rng, C // 2))[(o[g] + t) % 4]
    return {**numbers_of(rng), **stored(nx, pr), **weights(rng, f(rng, 128, 2048))}
def setup_inputs_spread(rng):
    d = setup_inputs(rng)
    d["x"] = big(wide(rng, N, 128, 4 * C, cols=6), 1)
    d["gh"] = big(wide(rng, N, 128, 4 * G, cols=6), 1)
    return d
def check_inputs(d):
    b = []
    for k in ("x", "gh", "u", "v"):
        a = np.abs(d[k].astype(np.float32))
        if not (np.isfinite(a).all() and ((a == 0) | (a >= 2.0 ** -30) & (a <= 2.0 ** 30)).all()): b.append("a value of " + k)
    for r in range(N):
        if (np.sort(gentries(d["nx"][r]), axis=1) != np.arange(C + G)).any(): b.append("nx of rank %d is no permutation in some group" % r)
        p = gentries(d["pr"][r]).reshape(8, R, C)
        if (p < 0).any() or (p >= C).any(): b.append("pr of rank %d out of range" % r)
        elif (np.take_along_axis(p, p, axis=2) != np.arange(C)).any(): b.append("pr of rank %d: a partner's partner is another column" % r)
    if (d["wc"] != d["wc"][:1]).any(): b.append("wc differs between ranks")
    s = [mx_ref.live(p) for p in d["ws"]]
    if any((p != s[0]).any() for p in s): b.append("ws differs between ranks")
    return b
def read(X, n):
    p = np.argsort(n, axis=1)
    return (gcols(X, n[:, :C]).astype(np.float32) + gcols(X, p[:, :C]).astype(np.float32)).astype(BF)
def reference(x, gh, u, v, nx, pr, wc, ws):
    w = pk(wc[0], ws[0])
    layer = [pick(w, np.arange(128 * b, 128 * b + 128)) for b in range(4)]
    qu = [mx_ref.quantize(u[r]) for r in range(N)]
    now = [np.concatenate([x[r], gh[r]], axis=1) for r in range(N)]
    link = [gentries(nx[r]) for r in range(N)]
    pair = [gentries(pr[r]).reshape(8, R, C) for r in range(N)]
    j = np.arange(C)
    for t in range(R):
        made = []
        for r in range(N):
            q = mx_ref.quantize(read(now[r], link[r]))
            s = mx_ref.matmul(qu[r], q)[::16] + np.float32(0.0)
            a, n = pair[r][:, t], link[r][:, :C]
            o = np.take_along_axis(s, a, axis=1)
            swap = (j < a) & (s < o) | (j > a) & (o < s)
            link[r] = np.concatenate([np.where(swap, np.take_along_axis(n, a, axis=1), n), link[r][:, C:]], axis=1)
            h = tile([np.maximum(mx_ref.matmul(layer[b], q), np.float32(0.0)) * np.float32(0.015625) for b in range(4)])
            made.append(decode(mx_ref.quantize(h)).astype(BF))
        for r in range(N):
            now[r] = np.concatenate([made[r], cut(made[r ^ (1 << t % L)], 0, 4 * G)], axis=1)
    y, nl = np.zeros((N, 128, C), np.float32), np.zeros((N, 8, C + G), np.float32)
    oc, osc = np.zeros((N, 128, 4 * C), np.uint8), np.zeros((N, 16, C), np.uint8)
    for r in range(N):
        q = mx_ref.quantize(read(now[r], link[r]))
        y[r] = mx_ref.matmul(mx_ref.quantize(v[r]), q)
        nl[r] = link[r]
        oc[r], osc[r] = emit(q)
    return {"y": y, "nl": nl, "oc": oc, "osc": osc}

@@ -1,0 +1,366 @@
+from concourse.mybir import dt, AluOpType, ActivationFunctionType
+
+C, G, ROUNDS = 448, 256, 3
+WC = C + G
+K = WC * 4
+BIG = 1048576.0
+F32, BF16, I32, U16, U8, FP8 = "float32", "bfloat16", "int32", "uint16", "uint8", "float8_e4m3fn_x4"
+LA, LB = "ssss", "sssv"
+DA, DB, DG = "sssv", "vvss", ("sssv", "sssv", "svsv")
+
+SCRATCH = {
+    "nxi": ("sbuf", [128, 44], I32), "pri": ("sbuf", [128, 84], I32),
+    "nx16": ("sbuf", [128, 44], U16), "pr16": ("sbuf", [128, 84], U16),
+    "n4": ("sbuf", [128, 112], U16), "p4": ("sbuf", [128, 112], U16), "pv0": ("sbuf", [128, 28], U16),
+    "wq": ("sbuf", [128, 512], FP8), "wsc": ("sbuf", [128, 512], U8),
+    "ut": ("sbuf", [128, 512], BF16), "uq0": ("sbuf", [128, 128], FP8), "us0": ("sbuf", [128, 128], U8),
+    "uq": ("sbuf", [128, 128], FP8), "us": ("sbuf", [128, 128], U8), "uof": ("sbuf", [128, 8], U16),
+    "vt": ("sbuf", [128, 512], BF16), "vq": ("sbuf", [128, 128], FP8), "vs": ("sbuf", [128, 128], U8),
+    "et": ("sbuf", [128, 2048], BF16), "eo": ("sbuf", [128, 2048], BF16),
+    "eq": ("sbuf", [128, 512], FP8), "es": ("sbuf", [128, 512], U8),
+    "xi": ("sbuf", [128, C], I32), "xm": ("sbuf", [128, C], I32),
+    "db0": ("sbuf", [128, C], F32), "db": ("sbuf", [128, C], F32), "db2": ("sbuf", [128, C], BF16),
+    "pci": ("sbuf", [128, 8], I32), "qci": ("sbuf", [128, 8], I32), "qcf": ("sbuf", [128, 8], F32),
+    "colb": ("sbuf", [128, 8], F32), "col2": ("sbuf", [128, 8], F32),
+    "uoi": ("sbuf", [128, 8], I32), "i84": ("sbuf", [128, 84], F32), "jw": ("sbuf", [128, 84], F32),
+    "prf": ("sbuf", [128, 84], F32), "pd": ("sbuf", [128, 84], F32), "sgp": ("sbuf", [128, 84], F32), "kap": ("sbuf", [128, 84], F32),
+    "iota": ("sbuf", [128, WC], F32), "sigr": ("sbuf", [128, WC], F32),
+    "inv": ("sbuf", [128, WC], F32), "nxr0": ("sbuf", [128, WC], F32), "pvf": ("sbuf", [128, 28], F32),
+    "sb": ("sbuf", [128, 2 * C], F32), "l16": ("sbuf", [128, 168], U16),
+    "smf": ("sbuf", [128, 28], F32), "smm": ("sbuf", [128, 28], F32), "sms": ("sbuf", [128, 28], F32),
+    "sig": ("sbuf", [128, 28], U16),
+    "ysb": ("sbuf", [128, C], F32), "ps": ("psum", [128, 4096], F32),
+}
+for _t in range(4):
+    SCRATCH["win%d" % _t] = ("sbuf", [128, K], BF16)
+    SCRATCH["pb%d" % _t] = ("sbuf", [128, 4 * C], BF16)
+    SCRATCH["z%d" % _t] = ("sbuf", [128, 4 * C], BF16)
+    SCRATCH["zq%d" % _t] = ("sbuf", [128, C], FP8)
+    SCRATCH["zs%d" % _t] = ("sbuf", [128, C], U8)
+for _t in range(3):
+    SCRATCH["h%d" % _t] = ("sbuf", [128, 4 * C], BF16)
+    SCRATCH["hq%d" % _t] = ("sbuf", [128, C], FP8)
+    SCRATCH["hs%d" % _t] = ("sbuf", [128, C], U8)
+    SCRATCH["gq%d" % _t] = ("sbuf", [128, G], FP8)
+    SCRATCH["gs%d" % _t] = ("sbuf", [128, G], U8)
+    SCRATCH["nxr%d" % (_t + 1)] = ("sbuf", [128, C], F32)
+    SCRATCH["pvr%d" % _t] = ("sbuf", [128, C], F32)
+    SCRATCH["ssb%d" % _t] = ("sbuf", [128, C], F32)
+    SCRATCH["ssc%d" % _t] = ("sbuf", [128, C], F32)
+    SCRATCH["dif%d" % _t] = ("sbuf", [128, C], F32)
+    SCRATCH["sgn%d" % _t] = ("sbuf", [128, C], BF16)
+    SCRATCH["scd%d" % _t] = ("sbuf", [128, C], BF16)
+
+SEMAPHORES = ["cv", "cs", "cp", "cg", "sent", "st"] + ["ld%d" % i for i in range(8)] + ["arr%d" % t for t in range(3)]
+
+
+def R(name, lo, hi, step=1):
+    return (name, lo, hi, step)
+
+
+def rank_program(g, core, T, topo):
+    rank = T.rank_of(core)
+    if rank is None:
+        return
+    A_, F_ = AluOpType, ActivationFunctionType
+    eng = {"v": g.vector, "s": g.scalar, "p": g.tensor, "g": g, "y": g.sync}
+    csem = {"v": "cv", "s": "cs", "p": "cp", "g": "cg"}
+    issued, waited = {}, {}
+    known = {q: {} for q in eng}
+    snap = {}
+    log = {}
+
+    def clash(a, lo, hi, step):
+        if a[1] <= lo or hi <= a[0]: return False
+        return not (a[2] == step and step > 1 and (a[0] - lo) % step)
+
+    def region(r):
+        if r[0] == "ps": return ("bank%d" % (r[1] // 512), 0, 512, 1)
+        return r
+
+    def order(q, reads, writes):
+        need = {}
+        for rs, wr in ((reads, False), (writes, True)):
+            for r in rs:
+                n, lo, hi, step = region(r)
+                for a in log.get(n, []):
+                    if (wr or a[3]) and clash(a, lo, hi, step):
+                        s, v = a[4]
+                        need[s] = max(need.get(s, 0), v)
+        kn = known[q]
+        todo = [(s, v) for s, v in need.items() if kn.get(s, 0) < v]
+        for s, v in todo:
+            if any(s2 != s and snap.get((s2, v2), {}).get(s, 0) >= v for s2, v2 in todo): continue
+            eng[q].wait_ge(T.sem[s], v)
+            waited[s] = max(waited.get(s, 0), v)
+        for s, v in todo:
+            for s2, v2 in snap.get((s, v), {}).items(): kn[s2] = max(kn.get(s2, 0), v2)
+            kn[s] = max(kn.get(s, 0), v)
+
+    def note(tok, reads, writes):
+        for rs, wr in ((reads, False), (writes, True)):
+            for r in rs:
+                n, lo, hi, step = region(r)
+                w = wr or n[:4] == "bank"
+                l = log.setdefault(n, [])
+                if w and step == 1: l[:] = [a for a in l if not (lo <= a[0] and a[1] <= hi)]
+                l.append((lo, hi, step, w, tok))
+
+    def run(q, reads, writes, emit, sem=None, inc=1):
+        order(q, reads, writes)
+        s = sem or csem[q]
+        ins = emit()
+        issued[s] = issued.get(s, 0) + inc
+        ins.then_inc(T.sem[s], inc)
+        snap[(s, issued[s])] = dict(known[q])
+        note((s, issued[s]), reads, writes)
+
+    def ap(r):
+        if r[0] == "@": return ap(r[1]).indirect(ap(r[2]))
+        n, lo, hi, step = r
+        return T[n][:, lo:hi] if step == 1 else T[n][:, lo:hi:step]
+
+    def ind(win, off): return ("@", win, off)
+
+    def flat(rs):
+        o = []
+        for r in rs: o += [r[1], r[2]] if r[0] == "@" else [r]
+        return o
+    V = g.vector
+
+    def tt(out, a, b, op): run("v", flat([a, b]), [out], lambda: V.tensor_tensor(ap(out), ap(a), ap(b), op))
+
+    def tc(out, a):
+        w = out[1] if out[0] == "@" else out
+        run("v", flat([a]) + ([out[2]] if out[0] == "@" else []), [w], lambda: V.tensor_copy(ap(out), ap(a)))
+
+    def ts(out, a, s1, s2, op0, op1=None):
+        col = [s1] if isinstance(s1, tuple) else []
+        v1 = ap(s1) if col else s1
+        if op1 is None: run("v", [a] + col, [out], lambda: V.tensor_scalar(ap(out), ap(a), v1, None, op0))
+        else: run("v", [a] + col, [out], lambda: V.tensor_scalar(ap(out), ap(a), v1, s2, op0, op1))
+
+    def scan(out, d0, d1, op0, op1):
+        run("v", [d0, d1], [out], lambda: V.tensor_tensor_scan(ap(out), ap(d0), ap(d1), 0.0, op0, op1))
+
+    def act(out, a, fn=F_.Copy, scale=1.0, bias=0.0):
+        S = g.scalar
+        if isinstance(bias, tuple): run("s", flat([a, bias]), [out], lambda: S.activation(ap(out), ap(a), fn, bias=ap(bias)))
+        elif scale != 1.0 and bias != 0.0: run("s", flat([a]), [out], lambda: S.activation(ap(out), ap(a), fn, bias=bias, scale=scale))
+        elif scale != 1.0: run("s", flat([a]), [out], lambda: S.activation(ap(out), ap(a), fn, scale=scale))
+        elif bias != 0.0: run("s", flat([a]), [out], lambda: S.activation(ap(out), ap(a), fn, bias=bias))
+        else: run("s", flat([a]), [out], lambda: S.activation(ap(out), ap(a), fn))
+
+    def copy(q, out, a):
+        if q == "s": act(out, a)
+        else: tc(out, a)
+
+    def quant(q, s, t, a, b):
+        run("v", [R(t, 4 * a, 4 * b)], [R(q, a, b), R(s, a, b)], lambda: V.quantize_mx(T[q][:, a:b], T[s][:, a:b], T[t][:, 4 * a:4 * b]))
+
+    bank = [0]
+
+    def mm(wq, ws, wa, xq, xs, a, b):
+        k = bank[0] % 8
+        bank[0] += 1
+        o = R("ps", 512 * k, 512 * k + b - a)
+        run("p", [R(wq, wa, wa + 128), R(ws, wa, wa + 128), R(xq, a, b), R(xs, a, b)], [o],
+            lambda: g.tensor.matmul_mx(ap(o), T[wq][:, wa:wa + 128], T[ws][:, wa:wa + 128], T[xq][:, a:b], T[xs][:, a:b], True, True))
+        return o
+
+    def iota(name, lo, hi, pattern, base, cm):
+        o = R(name, lo, hi)
+        if SCRATCH[name][2] == F32: run("g", [], [o], lambda: g.iota(ap(o), pattern, base, cm, allow_small_or_imprecise_dtypes=True))
+        else: run("g", [], [o], lambda: g.iota(ap(o), pattern, base, cm))
+
+    nld = [0]
+
+    def load(q, r, dst, src):
+        s = "ld%d" % nld[0]
+        nld[0] += 1
+        run(q, [], [r], lambda: eng[q].dma_start(dst, src), sem=s, inc=16)
+
+    def store(q, r, dst, src):
+        run(q, [r], [], lambda: eng[q].dma_start(dst, src), sem="st", inc=16)
+
+    load("y", R("nxi", 0, 44), T.nxi[:], T.nx[:])
+    load("y", R("win0", 0, 4 * C), T.win0[:, 0:4 * C], T.x[:])
+    load("y", R("win0", 4 * C, K), T.win0[:, 4 * C:K], T.gh[:])
+    load("y", R("ut", 0, 512), T.ut[:], T.u[:])
+    load("y", R("wq", 0, 512), T.wq[:, 0:512].bitcast(dt.uint8), T.wc[:])
+    load("y", R("wsc", 0, 512), T.wsc[:], T.ws[:])
+    load("y", R("pri", 0, 84), T.pri[:], T.pr[:])
+    load("y", R("vt", 0, 512), T.vt[:], T.v[:])
+
+    iota("pci", 0, 1, [[0, 1]], 0, 1)
+    iota("xi", 0, C, [[0, 28], [1, 16]], 128, -1)
+    iota("iota", 0, WC, [[1, WC]], 0, 0)
+    iota("uoi", 0, 8, [[16, 8]], 0, 0)
+    iota("i84", 0, 84, [[0, 3], [16, 28]], 0, 0)
+    run("v", [], [R("et", 0, 2048)], lambda: V.memset(T.et[:], 1.0))
+    run("g", [R("et", 0, 2048)], [R("eo", 0, 2048)],
+        lambda: g.affine_select(T.eo[:], T.et[:], [[-1, 4], [1, 512]], A_.is_equal, 0.0, 0, -4))
+    iota("sigr", C, WC, [[1, G]], C, 0)
+    ts(R("qci", 0, 1), R("pci", 0, 1), 15, None, A_.bitwise_and)
+    tc(R("qcf", 0, 1), R("qci", 0, 1))
+    ts(R("colb", 0, 1), R("qcf", 0, 1), -BIG, 15.0 * BIG, A_.mult, A_.add)
+    ts(R("xm", 0, C), R("xi", 0, C), 15, None, A_.bitwise_and)
+    ts(R("db0", 0, C), R("xm", 0, C), 0.0, -32.0 * BIG, A_.is_equal, A_.mult)
+    act(R("db", 0, C), R("db0", 0, C), bias=BIG)
+    act(R("db2", 0, C), R("db0", 0, C), scale=2.0 / BIG, bias=2.0)
+    act(R("jw", 0, 84), R("i84", 0, 84), F_.Identity, bias=R("qcf", 0, 1))
+    tc(R("nx16", 0, 44), R("nxi", 0, 44))
+    for e in range(4): ts(R("n4", 28 * e, 28 * e + 28), R("nxi", 0, 28), 4.0, float(e), A_.mult, A_.add)
+    tc(ind(R("inv", 0, WC), R("nx16", 0, 44)), R("iota", 0, WC))
+    scan(R("sb", 0, C), R("db", 0, C), R("inv", 0, C), A_.add, A_.max)
+    ts(R("pvf", 0, 28), R("sb", 15, C, 16), R("colb", 0, 1), None, A_.subtract)
+    for e in range(4): ts(R("p4", 28 * e, 28 * e + 28), R("pvf", 0, 28), 4.0, float(e), A_.mult, A_.add)
+    act(R("nxr0", 0, WC), ind(R("iota", 0, WC), R("nx16", 0, 44)))
+    store("y", R("nxr0", C, WC), T.nl[:, C:WC], T.nxr0[0:128:16, C:WC])
+
+    def scorer():
+        tc(R("pv0", 0, 28), R("pvf", 0, 28))
+        tc(R("uof", 0, 8), R("uoi", 0, 8))
+        quant("uq0", "us0", "ut", 0, 128)
+        run("v", [R("uq0", 0, 128), R("uof", 0, 8)], [R("uq", 0, 128)],
+            lambda: V.tensor_copy(T.uq[:, 0:128].bitcast(dt.uint32), T.uq0[:, 0:128].bitcast(dt.uint32).indirect(T.uof[:, 0:8])))
+        run("s", [R("us0", 0, 128), R("uof", 0, 8)], [R("us", 0, 128)],
+            lambda: g.scalar.activation(T.us[:, 0:128], T.us0[:, 0:128].indirect(T.uof[:, 0:8]), F_.Copy))
+        tc(R("pr16", 0, 84), R("pri", 0, 84))
+
+    def partners():
+        tc(R("prf", 0, 84), R("pri", 0, 84))
+        tt(R("pd", 0, 84), R("prf", 0, 84), R("jw", 0, 84), A_.subtract)
+        ts(R("col2", 0, 1), R("qcf", 0, 1), -2.0, 30.0, A_.mult, A_.add)
+
+    AB = ((0, G), (G, C))
+    HALVES = ((0, C // 2), (C // 2, C))
+
+    def windows(t, e):
+        return R("win0", 0, K) if t == 0 else R("win%d" % t, WC * e, WC * e + WC)
+
+    def offs(t, e, which, a, b):
+        a, b = a // 16, b // 16
+        if t == 0: return R("n4" if which == 0 else "p4", 28 * e + a, 28 * e + b)
+        o = 56 * (t - 1) + 28 * which
+        return R("l16", o + a, o + b)
+
+    def fetch(t, ch):
+        a, b = AB[ch]
+        for e in range(4): act(R("pb%d" % t, C * e + a, C * e + b), ind(windows(t, e), offs(t, e, 0, a, b)))
+
+    def addup(t, ch):
+        a, b = AB[ch]
+        for e in range(4): tt(R("z%d" % t, 4 * a + e, 4 * b, 4), ind(windows(t, e), offs(t, e, 1, a, b)), R("pb%d" % t, C * e + a, C * e + b), A_.add)
+        quant("zq%d" % t, "zs%d" % t, "z%d" % t, a, b)
+
+    def layer(t, ch):
+        a, b = AB[ch]
+        return [mm("wq", "wsc", 128 * k, "zq%d" % t, "zs%d" % t, a, b) for k in range(4)]
+
+    def score(t, ch):
+        a, b = AB[ch]
+        return mm("uq", "us", 0, "zq%d" % t, "zs%d" % t, a, b)
+
+    def relu(q, t, ch, k, o):
+        a, b = AB[ch]
+        out = R("h%d" % t, 4 * a + k, 4 * b, 4)
+        if q == "s": act(out, o, F_.Relu, scale=0.015625)
+        else: ts(out, o, 0.0, 0.015625, A_.max, A_.mult)
+
+    def unpack(t, src, a, b):
+        return [mm("eq", "es", 128 * k, ("gq%d" if src else "hq%d") % t, ("gs%d" if src else "hs%d") % t, a, b) for k in range(4)]
+
+    def keep(q, t, k, o, a):
+        copy(q, R("win%d" % (t + 1), WC * k + a, WC * k + a + o[2] - o[1]), o)
+
+    def send(t):
+        dst = T.cores[rank ^ (1 << t)]
+        rid, pid, _ = topo.addr(dst)
+        e = topo.engines(core, dst)[:8]
+        m = sum(1 << i for i in e)
+        h, s = "hq%d" % t, "hs%d" % t
+        order("g", [R(h, 0, G), R(s, 0, G)], [])
+        g.remote_dma(T["gq%d" % t][:, 0:G].bitcast(dt.uint8), T[h][:, 0:G].bitcast(dt.uint8), T.sem["arr%d" % t], T.sem.sent, pid, rid, m)
+        g.remote_dma(T["gs%d" % t][:, 0:G], T[s][:, 0:G], T.sem["arr%d" % t], T.sem.sent, pid, rid, m)
+        issued["sent"] = issued.get("sent", 0) + 2 * len(e)
+        tok = ("arr%d" % t, 2 * len(e))
+        issued[tok[0]] = tok[1]
+        note(tok, [], [R("gq%d" % t, 0, G), R("gs%d" % t, 0, G)])
+
+    for t in range(ROUNDS):
+        nr = "nxr%d" % (t + 1)
+        w = (28 * t, 28 * t + 28)
+        ssb, ssc, dif, sgn, scd, pvr = ["%s%d" % (n, t) for n in ("ssb", "ssc", "dif", "sgn", "scd", "pvr")]
+        fetch(t, 0)
+        addup(t, 0)
+        la = layer(t, 0)
+        if t: s0 = score(t, 0)
+        fetch(t, 1)
+        addup(t, 1)
+        if t: s1 = score(t, 1)
+        for k in range(4): relu(LA[k], t, 0, k, la[k])
+        quant("hq%d" % t, "hs%d" % t, "h%d" % t, 0, G)
+        send(t)
+        if t == 0:
+            scorer()
+            s0 = score(t, 0)
+            s1 = score(t, 1)
+            quant("eq", "es", "eo", 0, 512)
+        lb = layer(t, 1)
+        act(R(ssb, 0, G), s0)
+        tc(R(ssc, G, C), s1)
+        act(R(ssb, G, C), s1)
+        tc(R(ssc, 0, G), s0)
+        da = unpack(t, 0, 0, G)
+        for a, b in HALVES:
+            tt(R(dif, a, b), ind(R(ssb, 0, C), R("pr16", 28 * t + a // 16, 28 * t + b // 16)), R(ssc, a, b), A_.subtract)
+        if t == 0: partners()
+        for k in (0, 1): relu(LB[k], t, 1, k, lb[k])
+        for a, b in HALVES: act(R(sgn, a, b), R(dif, a, b), F_.Sign)
+        if t == 0:
+            act(R("sgp", 0, 84), R("pd", 0, 84), F_.Sign)
+            act(R("kap", 0, 84), R("sgp", 0, 84), F_.Identity, bias=R("col2", 0, 1))
+        for k in (2, 3): relu(LB[k], t, 1, k, lb[k])
+        for a, b in HALVES: scan(R(scd, a, b), R("db2", a, b), R(sgn, a, b), A_.add, A_.max)
+        tt(R("smf", 0, 28), R(scd, 15, C, 16), R("kap", *w), A_.is_equal)
+        tt(R("smm", 0, 28), R("smf", 0, 28), R("pd", *w), A_.mult)
+        tt(R("sms", 0, 28), R("smm", 0, 28), R("jw", 0, 28), A_.add)
+        tc(R("sig", 0, 28), R("sms", 0, 28))
+        quant("hq%d" % t, "hs%d" % t, "h%d" % t, G, C)
+        db = unpack(t, 0, G, C)
+        for k in range(4):
+            if DA[k] == "s": keep("s", t, k, da[k], 0)
+        act(R("sigr", 0, C), ind(R("iota", 0, C), R("sig", 0, 28)))
+        act(R(nr, 0, C), ind(R("nxr%d" % t, 0, C), R("sig", 0, 28)))
+        for k in range(4):
+            if DA[k] == "v": keep("v", t, k, da[k], 0)
+        for k in range(4):
+            if DB[k] == "v": keep("v", t, k, db[k], G)
+        pv = R("pv0", 0, 28) if t == 0 else R("l16", 56 * t - 28, 56 * t)
+        tc(R(pvr, 0, C), ind(R("sigr", 0, WC), pv))
+        scan(R("sb", 0, C), R("db", 0, C), R(nr, 0, C), A_.add, A_.max)
+        ts(R("l16", 56 * t, 56 * t + 28), R("sb", 15, C, 16), R("colb", 0, 1), None, A_.subtract)
+        for k in range(4):
+            if DB[k] == "s": keep("s", t, k, db[k], G)
+        scan(R("sb", C, 2 * C), R("db", 0, C), R(pvr, 0, C), A_.add, A_.max)
+        ts(R("l16", 56 * t + 28, 56 * t + 56), R("sb", C + 15, 2 * C, 16), R("colb", 0, 1), None, A_.subtract)
+        if t == 2: quant("vq", "vs", "vt", 0, 128)
+        dg = unpack(t, 1, 0, G)
+        for k in range(4): keep(DG[t][k], t, k, dg[k], C)
+    store("y", R("nxr3", 0, C), T.nl[:, 0:C], T.nxr3[0:128:16, 0:C])
+    fetch(3, 0)
+    addup(3, 0)
+    ya = mm("vq", "vs", 0, "zq3", "zs3", 0, G)
+    store("y", R("zq3", 0, G), T.oc[:, 0:4 * G], T.zq3[:, 0:G].bitcast(dt.uint8))
+    fetch(3, 1)
+    act(R("ysb", 0, G), ya)
+    store("y", R("ysb", 0, G), T.y[:, 0:G], T.ysb[:, 0:G])
+    addup(3, 1)
+    yb = mm("vq", "vs", 0, "zq3", "zs3", G, C)
+    for k in range(4): store("y", R("zs3", 0, C), T.osc[4 * k:4 * k + 4, 0:C], T.zs3[32 * k:32 * k + 4, 0:C])
+    store("s", R("zq3", G, C), T.oc[:, 4 * G:4 * C], T.zq3[:, G:C].bitcast(dt.uint8))
+    act(R("ysb", G, C), yb)
+    store("s", R("ysb", G, C), T.y[:, G:C], T.ysb[:, G:C])
+    for s in sorted(issued):
+        if waited.get(s, 0) < issued[s]: (g if s == "sent" else g.sync).wait_ge(T.sem[s], issued[s])

@@ -3,32 +3,36 @@ from concourse.mybir import dt, AluOpType, ActivationFunctionType
 C, G, ROUNDS = 448, 256, 3
 WC = C + G
 K = WC * 4
-BIG = 1048576.0
-F32, BF16, I32, U16, U8, FP8 = "float32", "bfloat16", "int32", "uint16", "uint8", "float8_e4m3fn_x4"
-LA, LB = "ssss", "sssv"
-DA, DB, DG = "sssv", "vvss", ("sssv", "sssv", "svsv")
+UP = 1024.0
+F32, BF16, F16, I32, U16, U8, FP8 = "float32", "bfloat16", "float16", "int32", "uint16", "uint8", "float8_e4m3fn_x4"
+CFG = {
+    "read": [(0, 128, G, C)] * 3 + [(0, 128, 320, C)],
+    "layer": [(0, 128, G, C)] * 3, "send": [(0, 128, G), (0, G), (0, 128, G)],
+    "sr": [(0, 224, C)] * 3, "nr": [(0, C)] * 3, "pr": [(0, C)] * 4,
+    "score": [(0, G, C)] * 3, "pair": [(0, 224, C)] * 3, "bits": [(0, C)] * 3, "own": [(0, G, C)] * 3,
+}
+ORDER = """
+Lnx:y Lx:y Lgh:y Lpr:y Lw:y Lws:y Lu:y ones:v Ip:g qh:v qq:v I16:g ql:v q:v I4:g Iu:g Ij:g qf:v uof:v na:v nb:v nc:s ca:v c4:s I84:g unit0:g unit1:g unit2:g unit3:g Ig:g c16:v q16:v nd:v c40:s d4:s nx16:v nxa:s d16:s n42:v jw:s f002:s n41:v inv:v n40:v n43:v f001:s f000:s p400s:v f003:s f013:s pd:v f011:s f012:s p400o:v f010:v f023:s f021:s a00:v f022:s hi:v qz00:v r001:s r002:s r000:s f020:s a01:v r003:v qz01:v qh00:v sc00:g qu:v r013:s r010:s a02:v uq:v r012:s cpd:s qz02:v us:s r011:s s00:s lo:v s01:s qh01:v sc01:g ss00:g lh:v r020:s lo01:s lo00:s Lv:y r022:s qe:v r023:s p0s0:v hi01:v hi00:v r021:s k002:s k001:s base:v b00:v p0o0:v sm0:v sa0:v sg0:v k003:s k000:s qh02:v nr00:s sr01:v k010:v k011:v sr00:s n10s:v k013:s k012:v g002:s n10o:v g001:s g000:v g003:s f10:s f11:s f12:s pr00:v p410s:v p410o:v a10:v a11:v qz10:v r101:s qz11:v r102:s a12:v r100:s r110:v qz12:v r103:s r111:s qh10:v r113:s r112:s qh11:v sc10:g ss10:g s10:s p1s0:v s11:s lo10:s r122:v lo11:v r120:s hi10:v r121:s r123:s k100:s hi11:v k102:s b10:v qh12:v sm1:v k101:s p1o0:v sa1:v k103:s k110:v k112:s sg1:v nr10:s k113:v sr11:v k111:s sr10:v g103:s n20s:v g102:v g101:s n20o:v g100:s f20:s f21:s f22:s pr10:v p420s:v p420o:v a20:v qz20:v r201:s r203:s a21:v r202:v r200:s qz21:v r210:s r212:s r213:s r211:s s20:s qh20:v sc20:g a22:v qh21:v sc21:g ss20:g k202:s qz22:v p2s0:v s21:v r222:s lo21:s lo20:v r220:v hi20:v hi21:v r221:s r223:s k203:s qh22:v b20:v p2o0:v sm2:v k200:s sa2:v k201:s k211:s sg2:v sr20:v k213:s k212:s sr21:s k210:v nr20:s Sna:y g201:s pr20:v g202:s n30s:v g200:v g203:s n30o:v p430s:v f30:s p430o:v f31:s qv:v a30:v qz30:v Sc0:y f32:s y0:s Sy0:y nxb:s Snb:y a31:v qz31:v Sc1:y a32:v y1:s Sy1:y qz32:v Sc2:y Ss0:s Ss1:y Ss2:s Ss3:y y2:v Sy2:y
+"""
 
 SCRATCH = {
-    "nxi": ("sbuf", [128, 44], I32), "pri": ("sbuf", [128, 84], I32),
-    "nx16": ("sbuf", [128, 44], U16), "pr16": ("sbuf", [128, 84], U16),
-    "n4": ("sbuf", [128, 112], U16), "p4": ("sbuf", [128, 112], U16), "pv0": ("sbuf", [128, 28], U16),
+    "nxi": ("sbuf", [128, 44], I32), "pri": ("sbuf", [128, 84], I32), "nx16": ("sbuf", [128, 44], U16),
+    "n4": ("sbuf", [128, 112], U16),
     "wq": ("sbuf", [128, 512], FP8), "wsc": ("sbuf", [128, 512], U8),
     "ut": ("sbuf", [128, 512], BF16), "uq0": ("sbuf", [128, 128], FP8), "us0": ("sbuf", [128, 128], U8),
     "uq": ("sbuf", [128, 128], FP8), "us": ("sbuf", [128, 128], U8), "uof": ("sbuf", [128, 8], U16),
     "vt": ("sbuf", [128, 512], BF16), "vq": ("sbuf", [128, 128], FP8), "vs": ("sbuf", [128, 128], U8),
-    "et": ("sbuf", [128, 2048], BF16), "eo": ("sbuf", [128, 2048], BF16),
+    "et": ("sbuf", [128, 512], BF16), "eo": ("sbuf", [128, 2048], BF16),
     "eq": ("sbuf", [128, 512], FP8), "es": ("sbuf", [128, 512], U8),
-    "xi": ("sbuf", [128, C], I32), "xm": ("sbuf", [128, C], I32),
-    "db0": ("sbuf", [128, C], F32), "db": ("sbuf", [128, C], F32), "db2": ("sbuf", [128, C], BF16),
-    "pci": ("sbuf", [128, 8], I32), "qci": ("sbuf", [128, 8], I32), "qcf": ("sbuf", [128, 8], F32),
-    "colb": ("sbuf", [128, 8], F32), "col2": ("sbuf", [128, 8], F32),
+    "pci": ("sbuf", [128, 28], I32), "qci": ("sbuf", [128, 32], I32), "q16": ("sbuf", [128, 28], U16),
+    "col": ("sbuf", [128, 16], F32), "nar": ("sbuf", [128, 192], F32),
+    "d16": ("sbuf", [128, C], BF16), "d4": ("sbuf", [128, C], BF16),
     "uoi": ("sbuf", [128, 8], I32), "i84": ("sbuf", [128, 84], F32), "jw": ("sbuf", [128, 84], F32),
-    "prf": ("sbuf", [128, 84], F32), "pd": ("sbuf", [128, 84], F32), "sgp": ("sbuf", [128, 84], F32), "kap": ("sbuf", [128, 84], F32),
-    "iota": ("sbuf", [128, WC], F32), "sigr": ("sbuf", [128, WC], F32),
-    "inv": ("sbuf", [128, WC], F32), "nxr0": ("sbuf", [128, WC], F32), "pvf": ("sbuf", [128, 28], F32),
-    "sb": ("sbuf", [128, 2 * C], F32), "l16": ("sbuf", [128, 168], U16),
-    "smf": ("sbuf", [128, 28], F32), "smm": ("sbuf", [128, 28], F32), "sms": ("sbuf", [128, 28], F32),
-    "sig": ("sbuf", [128, 28], U16),
+    "lohi": ("sbuf", [128, 168], F32), "lh16": ("sbuf", [128, 168], U16),
+    "pd": ("sbuf", [128, 84], F32), "cpd": ("sbuf", [128, 84], F32), "base": ("sbuf", [128, 84], F32),
+    "iota": ("sbuf", [128, WC], F32), "inv": ("sbuf", [128, WC], F32), "nxr0": ("sbuf", [128, WC], F32),
+    "sigr": ("sbuf", [128, WC], F32),
+    "sm": ("sbuf", [128, 56 * 3], F32), "sig": ("sbuf", [128, 84], U16),
     "ysb": ("sbuf", [128, C], F32), "ps": ("psum", [128, 4096], F32),
 }
 for _t in range(4):
@@ -37,6 +41,9 @@ for _t in range(4):
     SCRATCH["z%d" % _t] = ("sbuf", [128, 4 * C], BF16)
     SCRATCH["zq%d" % _t] = ("sbuf", [128, C], FP8)
     SCRATCH["zs%d" % _t] = ("sbuf", [128, C], U8)
+    SCRATCH["sb%d" % _t] = ("sbuf", [128, 3 * C], F32)
+    SCRATCH["sh%d" % _t] = ("sbuf", [128, 3 * C], F16)
+    SCRATCH["l%d" % _t] = ("sbuf", [128, 252], U16)
 for _t in range(3):
     SCRATCH["h%d" % _t] = ("sbuf", [128, 4 * C], BF16)
     SCRATCH["hq%d" % _t] = ("sbuf", [128, C], FP8)
@@ -44,12 +51,11 @@ for _t in range(3):
     SCRATCH["gq%d" % _t] = ("sbuf", [128, G], FP8)
     SCRATCH["gs%d" % _t] = ("sbuf", [128, G], U8)
     SCRATCH["nxr%d" % (_t + 1)] = ("sbuf", [128, C], F32)
-    SCRATCH["pvr%d" % _t] = ("sbuf", [128, C], F32)
+    SCRATCH["pvr%d" % _t] = ("sbuf", [128, C], F16)
     SCRATCH["ssb%d" % _t] = ("sbuf", [128, C], F32)
-    SCRATCH["ssc%d" % _t] = ("sbuf", [128, C], F32)
-    SCRATCH["dif%d" % _t] = ("sbuf", [128, C], F32)
-    SCRATCH["sgn%d" % _t] = ("sbuf", [128, C], BF16)
-    SCRATCH["scd%d" % _t] = ("sbuf", [128, C], BF16)
+    SCRATCH["slo%d" % _t] = ("sbuf", [128, C], F32)
+    SCRATCH["bit%d" % _t] = ("sbuf", [128, C], BF16)
+    SCRATCH["scd%d" % _t] = ("sbuf", [128, C], F16)
 
 SEMAPHORES = ["cv", "cs", "cp", "cg", "sent", "st"] + ["ld%d" % i for i in range(8)] + ["arr%d" % t for t in range(3)]
 
@@ -58,35 +64,261 @@ def R(name, lo, hi, step=1):
     return (name, lo, hi, step)
 
 
-def rank_program(g, core, T, topo):
+def cuts(c):
+    return list(zip(c[:-1], c[1:]))
+
+
+def calls(g, core, T, topo, bank):
     rank = T.rank_of(core)
-    if rank is None:
-        return
     A_, F_ = AluOpType, ActivationFunctionType
+    V, S = g.vector, g.scalar
+    dq = {"y": g.sync, "s": g.scalar}
+    ops = []
+
+    def op(name, qs, reads, writes, emit, sem=None):
+        ops.append((name, qs, reads, writes, emit, sem))
+
+    def ap(r):
+        if r[0] == "@": return ap(r[1]).indirect(ap(r[2]))
+        if r[0] == "ps": return T.ps[:, 512 * bank[r[1]]:512 * bank[r[1]] + r[2]]
+        n, lo, hi, step = r
+        return T[n][:, lo:hi] if step == 1 else T[n][:, lo:hi:step]
+
+    def ind(win, off): return ("@", win, off)
+
+    def flat(rs):
+        o = []
+        for r in rs:
+            if isinstance(r, tuple): o += [r[1], r[2]] if r[0] == "@" else [r]
+        return o
+
+    def val(s): return ap(s) if isinstance(s, tuple) else s
+
+    def tt(n, out, a, b, o): op(n, "v", flat([a, b]), [out], lambda q: V.tensor_tensor(ap(out), ap(a), ap(b), o))
+
+    def tc(n, out, a): op(n, "v", flat([a]), [out], lambda q: V.tensor_copy(ap(out), ap(a)))
+
+    def ts(n, out, a, s1, s2, o0, o1=None):
+        if o1 is None: op(n, "v", flat([a, s1]), [out], lambda q: V.tensor_scalar(ap(out), ap(a), val(s1), None, o0))
+        else: op(n, "v", flat([a, s1, s2]), [out], lambda q: V.tensor_scalar(ap(out), ap(a), val(s1), val(s2), o0, o1))
+
+    def scan(n, out, d0, d1):
+        op(n, "v", [d0, d1], [out], lambda q: V.tensor_tensor_scan(ap(out), ap(d0), ap(d1), 0.0, A_.add, A_.max))
+
+    def copy(n, qs, out, a):
+        op(n, qs, flat([a]), [out], lambda q: S.activation(ap(out), ap(a), F_.Copy) if q == "s" else V.tensor_copy(ap(out), ap(a)))
+
+    def affine(n, qs, out, a, mul, add):
+        fn = F_.Identity if isinstance(add, tuple) else F_.Copy
+        op(n, qs, flat([a, add]), [out], lambda q: S.activation(ap(out), ap(a), fn, bias=val(add), scale=mul) if q == "s"
+           else V.tensor_scalar(ap(out), ap(a), mul, val(add), A_.mult, A_.add))
+
+    def relu(n, out, a):
+        op(n, "sv", [a], [out], lambda q: S.activation(ap(out), ap(a), F_.Relu, scale=0.015625) if q == "s"
+           else V.tensor_scalar(ap(out), ap(a), 0.0, 0.015625, A_.max, A_.mult))
+
+    def quant(n, q, s, t, a, b):
+        op(n, "v", [R(t, 4 * a, 4 * b)], [R(q, a, b), R(s, a, b)], lambda _: V.quantize_mx(T[q][:, a:b], T[s][:, a:b], T[t][:, 4 * a:4 * b]))
+
+    def mm(n, wq, ws, wa, xq, xs, a, b):
+        o = ("ps", n, b - a, 1)
+        op(n, "p", [R(wq, wa, wa + 128), R(ws, wa, wa + 128), R(xq, a, b), R(xs, a, b)], [o],
+           lambda q: g.tensor.matmul_mx(ap(o), T[wq][:, wa:wa + 128], T[ws][:, wa:wa + 128], T[xq][:, a:b], T[xs][:, a:b], True, True))
+        return o
+
+    def iota(n, name, lo, hi, pattern, base, cm):
+        o = R(name, lo, hi)
+        if SCRATCH[name][2] == F32: op(n, "g", [], [o], lambda q: g.iota(ap(o), pattern, base, cm, allow_small_or_imprecise_dtypes=True))
+        else: op(n, "g", [], [o], lambda q: g.iota(ap(o), pattern, base, cm))
+
+    nld = [0]
+
+    def load(n, r, dst, src):
+        op(n, "ys", [], [r], lambda q: dq[q].dma_start(dst, src), "ld%d" % nld[0])
+        nld[0] += 1
+
+    def store(n, r, dst, src):
+        op(n, "ys", [r], [], lambda q: dq[q].dma_start(dst, src), "st")
+
+    load("Lnx", R("nxi", 0, 44), T.nxi[:], T.nx[:])
+    load("Lx", R("win0", 0, 4 * C), T.win0[:, 0:4 * C], T.x[:])
+    load("Lgh", R("win0", 4 * C, K), T.win0[:, 4 * C:K], T.gh[:])
+    load("Lw", R("wq", 0, 512), T.wq[:, 0:512].bitcast(dt.uint8), T.wc[:])
+    load("Lws", R("wsc", 0, 512), T.wsc[:], T.ws[:])
+    load("Lu", R("ut", 0, 512), T.ut[:], T.u[:])
+    load("Lpr", R("pri", 0, 84), T.pri[:], T.pr[:])
+    load("Lv", R("vt", 0, 512), T.vt[:], T.v[:])
+
+    col = lambda k: R("col", k, k + 1)
+    Q, QH, QL, C16, CA, C4, C40 = [col(k) for k in range(7)]
+    iota("Ip", "pci", 0, 28, [[0, 28]], 0, 1)
+    iota("I16", "nar", 7, 32, [[1, 25]], -1, 0)
+    iota("I4", "nar", 32, 48, [[0, 4], [1, 4]], 0, 0)
+    iota("Ij", "iota", 0, WC, [[1, WC]], 0, 0)
+    iota("Iu", "uoi", 0, 8, [[16, 8]], 0, 0)
+    iota("I84", "i84", 0, 84, [[0, 3], [16, 28]], 0, 0)
+    op("ones", "v", [], [R("et", 0, 512)], lambda q: V.memset(T.et[:], 1.0))
+    for b in range(4):
+        op("unit%d" % b, "g", [R("et", 0, 512)], [R("eo", 512 * b, 512 * b + 512)],
+           lambda q, b=b: g.affine_select(T.eo[:, 512 * b:512 * b + 512], T.et[:], [[1, 512]], A_.is_equal, 0.0, -b, -4))
+    iota("Ig", "sigr", C, WC, [[1, G]], C, 0)
+    ts("q", R("qci", 0, 28), R("pci", 0, 28), 15, None, A_.bitwise_and)
+    ts("qh", R("qci", 29, 30), R("pci", 0, 1), 2, 3, A_.arith_shift_right, A_.bitwise_and)
+    ts("ql", R("qci", 30, 31), R("pci", 0, 1), 3, None, A_.bitwise_and)
+    ts("qq", R("qci", 28, 29), R("pci", 0, 1), 15, None, A_.bitwise_and)
+    tc("qf", R("col", 0, 3), R("qci", 28, 31))
+    tc("q16", R("q16", 0, 28), R("qci", 0, 28))
+    ts("na", R("nar", 55, 80), R("nar", 7, 32), Q, -4.0 * UP, A_.is_equal, A_.mult)
+    ts("nb", R("nar", 80, 96), R("nar", 32, 48), QH, -4.0 * UP, A_.is_equal, A_.mult)
+    affine("nc", "sv", R("nar", 104, 144), R("nar", 55, 95), -0.25, 0.0)
+    tt("nd", R("nar", 152, 192), R("nar", 56, 96), R("nar", 104, 144), A_.add)
+    copy("d4", "s", R("d4", 0, C), ind(R("nar", 176, 192), R("q16", 0, 28)))
+    copy("d16", "s", R("d16", 0, C), ind(R("nar", 152, 168), R("q16", 0, 28)))
+    ts("c16", C16, Q, 15.0, UP, A_.is_lt, A_.mult)
+    ts("ca", CA, QH, 3.0, UP, A_.is_lt, A_.mult)
+    affine("c4", "sv", C4, QL, -float(WC), CA)
+    affine("c40", "sv", C40, QL, -0.25, CA)
+    affine("jw", "sv", R("jw", 0, 84), R("i84", 0, 84), 1.0, Q)
+
+    def four(n, t, k, row, a, b):
+        sb = "sh%d" % t if t and k else "sb%d" % t
+        scan(n + "s", R(sb, C * k + a, C * k + b), R("d4", a, b), R(row, a, b))
+        o, s = R("l%d" % t, 112 * k + a // 4, 112 * k + b // 4), R(sb, C * k + a + 3, C * k + b, 4)
+        if t == 0: ts(n + "o", o, s, C40, 4.0, A_.subtract, A_.mult)
+        else: ts(n + "o", o, s, C4, None, A_.subtract)
+
+    def previous(t, row):
+        for i, (a, b) in enumerate(cuts(CFG["pr"][t])): four("p4%d%d" % (t, i), t, 1, row, a, b)
+        if t < ROUNDS:
+            sb = "sh%d" % t if t else "sb%d" % t
+            scan("p%ds0" % t, R(sb, 2 * C, 3 * C), R("d16", 0, C), R(row, 0, C))
+            ts("p%do0" % t, R("l%d" % t, 224, 252), R(sb, 2 * C + 15, 3 * C, 16), C16, None, A_.subtract)
+
+    tc("nx16", R("nx16", 0, 44), R("nxi", 0, 44))
+    for e in range(4): ts("n4%d" % e, R("n4", 28 * e, 28 * e + 28), R("nxi", 0, 28), 4.0, float(e), A_.mult, A_.add)
+    op("inv", "v", [R("nx16", 0, 44), R("iota", 0, WC)], [R("inv", 0, WC)],
+       lambda q: V.tensor_copy(T.inv[:, 0:WC].indirect(T.nx16[:, 0:44]), T.iota[:, 0:WC]))
+    previous(0, "inv")
+    copy("nxa", "sv", R("nxr0", 0, C), ind(R("iota", 0, WC), R("nx16", 0, 28)))
+    copy("nxb", "sv", R("nxr0", C, WC), ind(R("iota", 0, WC), R("nx16", 28, 44)))
+    store("Snb", R("nxr0", C, WC), T.nl[:, C:WC], T.nxr0[0:128:16, C:WC])
+    tc("uof", R("uof", 0, 8), R("uoi", 0, 8))
+    quant("qu", "uq0", "us0", "ut", 0, 128)
+    op("uq", "v", [R("uq0", 0, 128), R("uof", 0, 8)], [R("uq", 0, 128)],
+       lambda q: V.tensor_copy(T.uq[:, 0:128].bitcast(dt.uint32), T.uq0[:, 0:128].bitcast(dt.uint32).indirect(T.uof[:, 0:8])))
+    copy("us", "sv", R("us", 0, 128), ind(R("us0", 0, 128), R("uof", 0, 8)))
+    quant("qe", "eq", "es", "eo", 0, 512)
+    quant("qv", "vq", "vs", "vt", 0, 128)
+    tt("lo", R("lohi", 0, 84), R("pri", 0, 84), R("jw", 0, 84), A_.min)
+    tt("hi", R("lohi", 84, 168), R("pri", 0, 84), R("jw", 0, 84), A_.max)
+    tc("lh", R("lh16", 0, 168), R("lohi", 0, 168))
+    tt("pd", R("pd", 0, 84), R("pri", 0, 84), R("jw", 0, 84), A_.subtract)
+    op("cpd", "sv", [R("pd", 0, 84), C16], [R("cpd", 0, 84)], lambda q: S.activation(T.cpd[:], T.pd[:], F_.Identity, scale=ap(C16)) if q == "s"
+       else V.tensor_scalar(T.cpd[:], T.pd[:], ap(C16), None, A_.mult))
+    tt("base", R("base", 0, 84), R("jw", 0, 84), R("cpd", 0, 84), A_.subtract)
+
+    def reading(t):
+        w, l, pb, z = R("win%d" % t, 0, K), "l%d" % t, "pb%d" % t, "z%d" % t
+        for i, (a, b) in enumerate(cuts(CFG["read"][t])):
+            n = "%d%d" % (t, i)
+            if t == 0:
+                for e in range(4): copy("f%s%d" % (n, e), "sv", R(pb, 4 * a + e, 4 * b, 4), ind(w, R("n4", 28 * e + a // 16, 28 * e + b // 16)))
+            else: copy("f" + n, "sv", R(pb, 4 * a, 4 * b), ind(w, R(l, a // 4, b // 4)))
+            tt("a" + n, R(z, 4 * a, 4 * b), ind(w, R(l, 112 + a // 4, 112 + b // 4)), R(pb, 4 * a, 4 * b), A_.add)
+
+    def send(t):
+        dst = T.cores[rank ^ (1 << t)]
+        rid, pid, _ = topo.addr(dst)
+        e = topo.engines(core, dst)[:8]
+        m, pieces = sum(1 << i for i in e), cuts(CFG["send"][t])
+        h, s, gq, gs, arr = "hq%d" % t, "hs%d" % t, "gq%d" % t, "gs%d" % t, "arr%d" % t
+        sem = (arr, len(e), len(e) * (len(pieces) + 1))
+        for i, (a, b) in enumerate(pieces):
+            op("sc%d%d" % (t, i), "g", [R(h, a, b)], [R(gq, a, b)], lambda q, a=a, b=b: g.remote_dma(
+                T[gq][:, a:b].bitcast(dt.uint8), T[h][:, a:b].bitcast(dt.uint8), T.sem[arr], T.sem.sent, pid, rid, m), sem)
+        op("ss%d0" % t, "g", [R(s, 0, G)], [R(gs, 0, G)], lambda q: g.remote_dma(T[gs][:, 0:G], T[s][:, 0:G], T.sem[arr], T.sem.sent, pid, rid, m), sem)
+
+    for t in range(ROUNDS):
+        zq, zs, h, hq, hs, win = "zq%d" % t, "zs%d" % t, "h%d" % t, "hq%d" % t, "hs%d" % t, "win%d" % (t + 1)
+        ssb, slo, bit, scd, pvr, nr = "ssb%d" % t, "slo%d" % t, "bit%d" % t, "scd%d" % t, "pvr%d" % t, "nxr%d" % (t + 1)
+        reading(t)
+        for i, (a, b) in enumerate(cuts(CFG["layer"][t])):
+            n = "%d%d" % (t, i)
+            quant("qz" + n, zq, zs, "z%d" % t, a, b)
+            for k in range(4): relu("r%s%d" % (n, k), R(h, 4 * a + k, 4 * b, 4), mm("mw%s%d" % (n, k), "wq", "wsc", 128 * k, zq, zs, a, b))
+            quant("qh" + n, hq, hs, h, a, b)
+        send(t)
+        for i, (a, b) in enumerate(cuts(CFG["score"][t])): copy("s%d%d" % (t, i), "sv", R(ssb, a, b), mm("mu%d%d" % (t, i), "uq", "us", 0, zq, zs, a, b))
+        for i, (a, b) in enumerate(cuts(CFG["pair"][t])):
+            o = 28 * t + a // 16, 28 * t + b // 16
+            copy("lo%d%d" % (t, i), "sv", R(slo, a, b), ind(R(ssb, 0, C), R("lh16", *o)))
+            tt("hi%d%d" % (t, i), R(bit, a, b), ind(R(ssb, 0, C), R("lh16", 84 + o[0], 84 + o[1])), R(slo, a, b), A_.is_gt)
+        for i, (a, b) in enumerate(cuts(CFG["bits"][t])): scan("b%d%d" % (t, i), R(scd, a, b), R("d16", a, b), R(bit, a, b))
+        w = (28 * t, 28 * t + 28)
+        tt("sm%d" % t, R("sm", 56 * t, 56 * t + 28), R(scd, 15, C, 16), R("pd", *w), A_.mult)
+        tt("sa%d" % t, R("sm", 56 * t + 28, 56 * t + 56), R("sm", 56 * t, 56 * t + 28), R("base", *w), A_.add)
+        tc("sg%d" % t, R("sig", *w), R("sm", 56 * t + 28, 56 * t + 56))
+        for i, (a, b) in enumerate(cuts(CFG["sr"][t])):
+            copy("sr%d%d" % (t, i), "sv", R("sigr", a, b), ind(R("iota", 0, C), R("sig", 28 * t + a // 16, 28 * t + b // 16)))
+        for i, (a, b) in enumerate(cuts(CFG["nr"][t])):
+            copy("nr%d%d" % (t, i), "sv", R(nr, a, b), ind(R("nxr%d" % t, 0, C), R("sig", 28 * t + a // 16, 28 * t + b // 16)))
+            four("n%d%d" % (t + 1, i), t + 1, 0, nr, a, b)
+        for i, (a, b) in enumerate(cuts(CFG["pr"][t + 1])):
+            copy("pr%d%d" % (t, i), "v", R(pvr, a, b), ind(R("sigr", 0, WC), R("l%d" % t, 224 + a // 16, 224 + b // 16)))
+        previous(t + 1, pvr)
+        for i, (a, b) in enumerate(cuts(CFG["own"][t])):
+            for k in range(4): copy("k%d%d%d" % (t, i, k), "sv", R(win, WC * k + a, WC * k + b), mm("me%d%d%d" % (t, i, k), "eq", "es", 128 * k, hq, hs, a, b))
+        for k in range(4): copy("g%d0%d" % (t, k), "sv", R(win, WC * k + C, WC * k + WC), mm("mg%d0%d" % (t, k), "eq", "es", 128 * k, "gq%d" % t, "gs%d" % t, 0, G))
+    store("Sna", R("nxr3", 0, C), T.nl[:, 0:C], T.nxr3[0:128:16, 0:C])
+    reading(3)
+    for i, (a, b) in enumerate(cuts(CFG["read"][3])):
+        quant("qz3%d" % i, "zq3", "zs3", "z3", a, b)
+        store("Sc%d" % i, R("zq3", a, b), T.oc[:, 4 * a:4 * b], T.zq3[:, a:b].bitcast(dt.uint8))
+        copy("y%d" % i, "sv", R("ysb", a, b), mm("mv%d" % i, "vq", "vs", 0, "zq3", "zs3", a, b))
+        store("Sy%d" % i, R("ysb", a, b), T.y[:, a:b], T.ysb[:, a:b])
+    for k in range(4): store("Ss%d" % k, R("zs3", 0, C), T.osc[4 * k:4 * k + 4, 0:C], T.zs3[32 * k:32 * k + 4, 0:C])
+    return ops
+
+
+def clash(a, lo, hi, step):
+    if a[1] <= lo or hi <= a[0]: return False
+    return not (a[2] == step and step > 1 and (a[0] - lo) % step)
+
+
+def rank_program(g, core, T, topo):
+    if T.rank_of(core) is None:
+        return
+    bank = {}
+    ops = calls(g, core, T, topo, bank)
+    by = {o[0]: o for o in ops}
+    seq = []
+    for w in ORDER.split():
+        name, q = w.split(":")
+        if q != "p": seq += [(by[r[1]], "p") for r in by[name][2] if r[0] == "ps"] + [(by[name], q)]
+    assert len(seq) == len(ops) == len({o[0][0] for o in seq})
     eng = {"v": g.vector, "s": g.scalar, "p": g.tensor, "g": g, "y": g.sync}
     csem = {"v": "cv", "s": "cs", "p": "cp", "g": "cg"}
     issued, waited = {}, {}
     known = {q: {} for q in eng}
     snap = {}
     log = {}
-
-    def clash(a, lo, hi, step):
-        if a[1] <= lo or hi <= a[0]: return False
-        return not (a[2] == step and step > 1 and (a[0] - lo) % step)
+    free = list(range(8))
 
     def region(r):
-        if r[0] == "ps": return ("bank%d" % (r[1] // 512), 0, 512, 1)
-        return r
+        return ("bank%d" % bank[r[1]], 0, 512, 1) if r[0] == "ps" else r
 
-    def order(q, reads, writes):
+    for (name, qs, reads, writes, emit, sem), q in seq:
+        for r in writes:
+            if r[0] == "ps": bank[r[1]] = free.pop(0)
+        for r in reads:
+            if r[0] == "ps": free.append(bank[r[1]])
+        remote = isinstance(sem, tuple)
         need = {}
-        for rs, wr in ((reads, False), (writes, True)):
+        for rs, wr in ((reads, False), ([] if remote else writes, True)):
             for r in rs:
                 n, lo, hi, step = region(r)
                 for a in log.get(n, []):
-                    if (wr or a[3]) and clash(a, lo, hi, step):
-                        s, v = a[4]
-                        need[s] = max(need.get(s, 0), v)
+                    if (wr or a[3]) and clash(a, lo, hi, step): need[a[4][0]] = max(need.get(a[4][0], 0), a[4][1])
         kn = known[q]
         todo = [(s, v) for s, v in need.items() if kn.get(s, 0) < v]
         for s, v in todo:
@@ -96,8 +328,18 @@ def rank_program(g, core, T, topo):
         for s, v in todo:
             for s2, v2 in snap.get((s, v), {}).items(): kn[s2] = max(kn.get(s2, 0), v2)
             kn[s] = max(kn.get(s, 0), v)
-
-    def note(tok, reads, writes):
+        ins = emit(q)
+        if remote:
+            issued["sent"] = issued.get("sent", 0) + sem[1]
+            tok = (sem[0], sem[2])
+            issued[sem[0]] = sem[2]
+            reads = []
+        else:
+            s, inc = (sem, 16) if sem else (csem[q], 1)
+            issued[s] = issued.get(s, 0) + inc
+            ins.then_inc(T.sem[s], inc)
+            tok = (s, issued[s])
+            snap[tok] = dict(kn)
         for rs, wr in ((reads, False), (writes, True)):
             for r in rs:
                 n, lo, hi, step = region(r)
@@ -105,262 +347,5 @@ def rank_program(g, core, T, topo):
                 l = log.setdefault(n, [])
                 if w and step == 1: l[:] = [a for a in l if not (lo <= a[0] and a[1] <= hi)]
                 l.append((lo, hi, step, w, tok))
-
-    def run(q, reads, writes, emit, sem=None, inc=1):
-        order(q, reads, writes)
-        s = sem or csem[q]
-        ins = emit()
-        issued[s] = issued.get(s, 0) + inc
-        ins.then_inc(T.sem[s], inc)
-        snap[(s, issued[s])] = dict(known[q])
-        note((s, issued[s]), reads, writes)
-
-    def ap(r):
-        if r[0] == "@": return ap(r[1]).indirect(ap(r[2]))
-        n, lo, hi, step = r
-        return T[n][:, lo:hi] if step == 1 else T[n][:, lo:hi:step]
-
-    def ind(win, off): return ("@", win, off)
-
-    def flat(rs):
-        o = []
-        for r in rs: o += [r[1], r[2]] if r[0] == "@" else [r]
-        return o
-    V = g.vector
-
-    def tt(out, a, b, op): run("v", flat([a, b]), [out], lambda: V.tensor_tensor(ap(out), ap(a), ap(b), op))
-
-    def tc(out, a):
-        w = out[1] if out[0] == "@" else out
-        run("v", flat([a]) + ([out[2]] if out[0] == "@" else []), [w], lambda: V.tensor_copy(ap(out), ap(a)))
-
-    def ts(out, a, s1, s2, op0, op1=None):
-        col = [s1] if isinstance(s1, tuple) else []
-        v1 = ap(s1) if col else s1
-        if op1 is None: run("v", [a] + col, [out], lambda: V.tensor_scalar(ap(out), ap(a), v1, None, op0))
-        else: run("v", [a] + col, [out], lambda: V.tensor_scalar(ap(out), ap(a), v1, s2, op0, op1))
-
-    def scan(out, d0, d1, op0, op1):
-        run("v", [d0, d1], [out], lambda: V.tensor_tensor_scan(ap(out), ap(d0), ap(d1), 0.0, op0, op1))
-
-    def act(out, a, fn=F_.Copy, scale=1.0, bias=0.0):
-        S = g.scalar
-        if isinstance(bias, tuple): run("s", flat([a, bias]), [out], lambda: S.activation(ap(out), ap(a), fn, bias=ap(bias)))
-        elif scale != 1.0 and bias != 0.0: run("s", flat([a]), [out], lambda: S.activation(ap(out), ap(a), fn, bias=bias, scale=scale))
-        elif scale != 1.0: run("s", flat([a]), [out], lambda: S.activation(ap(out), ap(a), fn, scale=scale))
-        elif bias != 0.0: run("s", flat([a]), [out], lambda: S.activation(ap(out), ap(a), fn, bias=bias))
-        else: run("s", flat([a]), [out], lambda: S.activation(ap(out), ap(a), fn))
-
-    def copy(q, out, a):
-        if q == "s": act(out, a)
-        else: tc(out, a)
-
-    def quant(q, s, t, a, b):
-        run("v", [R(t, 4 * a, 4 * b)], [R(q, a, b), R(s, a, b)], lambda: V.quantize_mx(T[q][:, a:b], T[s][:, a:b], T[t][:, 4 * a:4 * b]))
-
-    bank = [0]
-
-    def mm(wq, ws, wa, xq, xs, a, b):
-        k = bank[0] % 8
-        bank[0] += 1
-        o = R("ps", 512 * k, 512 * k + b - a)
-        run("p", [R(wq, wa, wa + 128), R(ws, wa, wa + 128), R(xq, a, b), R(xs, a, b)], [o],
-            lambda: g.tensor.matmul_mx(ap(o), T[wq][:, wa:wa + 128], T[ws][:, wa:wa + 128], T[xq][:, a:b], T[xs][:, a:b], True, True))
-        return o
-
-    def iota(name, lo, hi, pattern, base, cm):
-        o = R(name, lo, hi)
-        if SCRATCH[name][2] == F32: run("g", [], [o], lambda: g.iota(ap(o), pattern, base, cm, allow_small_or_imprecise_dtypes=True))
-        else: run("g", [], [o], lambda: g.iota(ap(o), pattern, base, cm))
-
-    nld = [0]
-
-    def load(q, r, dst, src):
-        s = "ld%d" % nld[0]
-        nld[0] += 1
-        run(q, [], [r], lambda: eng[q].dma_start(dst, src), sem=s, inc=16)
-
-    def store(q, r, dst, src):
-        run(q, [r], [], lambda: eng[q].dma_start(dst, src), sem="st", inc=16)
-
-    load("y", R("nxi", 0, 44), T.nxi[:], T.nx[:])
-    load("y", R("win0", 0, 4 * C), T.win0[:, 0:4 * C], T.x[:])
-    load("y", R("win0", 4 * C, K), T.win0[:, 4 * C:K], T.gh[:])
-    load("y", R("ut", 0, 512), T.ut[:], T.u[:])
-    load("y", R("wq", 0, 512), T.wq[:, 0:512].bitcast(dt.uint8), T.wc[:])
-    load("y", R("wsc", 0, 512), T.wsc[:], T.ws[:])
-    load("y", R("pri", 0, 84), T.pri[:], T.pr[:])
-    load("y", R("vt", 0, 512), T.vt[:], T.v[:])
-
-    iota("pci", 0, 1, [[0, 1]], 0, 1)
-    iota("xi", 0, C, [[0, 28], [1, 16]], 128, -1)
-    iota("iota", 0, WC, [[1, WC]], 0, 0)
-    iota("uoi", 0, 8, [[16, 8]], 0, 0)
-    iota("i84", 0, 84, [[0, 3], [16, 28]], 0, 0)
-    run("v", [], [R("et", 0, 2048)], lambda: V.memset(T.et[:], 1.0))
-    run("g", [R("et", 0, 2048)], [R("eo", 0, 2048)],
-        lambda: g.affine_select(T.eo[:], T.et[:], [[-1, 4], [1, 512]], A_.is_equal, 0.0, 0, -4))
-    iota("sigr", C, WC, [[1, G]], C, 0)
-    ts(R("qci", 0, 1), R("pci", 0, 1), 15, None, A_.bitwise_and)
-    tc(R("qcf", 0, 1), R("qci", 0, 1))
-    ts(R("colb", 0, 1), R("qcf", 0, 1), -BIG, 15.0 * BIG, A_.mult, A_.add)
-    ts(R("xm", 0, C), R("xi", 0, C), 15, None, A_.bitwise_and)
-    ts(R("db0", 0, C), R("xm", 0, C), 0.0, -32.0 * BIG, A_.is_equal, A_.mult)
-    act(R("db", 0, C), R("db0", 0, C), bias=BIG)
-    act(R("db2", 0, C), R("db0", 0, C), scale=2.0 / BIG, bias=2.0)
-    act(R("jw", 0, 84), R("i84", 0, 84), F_.Identity, bias=R("qcf", 0, 1))
-    tc(R("nx16", 0, 44), R("nxi", 0, 44))
-    for e in range(4): ts(R("n4", 28 * e, 28 * e + 28), R("nxi", 0, 28), 4.0, float(e), A_.mult, A_.add)
-    tc(ind(R("inv", 0, WC), R("nx16", 0, 44)), R("iota", 0, WC))
-    scan(R("sb", 0, C), R("db", 0, C), R("inv", 0, C), A_.add, A_.max)
-    ts(R("pvf", 0, 28), R("sb", 15, C, 16), R("colb", 0, 1), None, A_.subtract)
-    for e in range(4): ts(R("p4", 28 * e, 28 * e + 28), R("pvf", 0, 28), 4.0, float(e), A_.mult, A_.add)
-    act(R("nxr0", 0, WC), ind(R("iota", 0, WC), R("nx16", 0, 44)))
-    store("y", R("nxr0", C, WC), T.nl[:, C:WC], T.nxr0[0:128:16, C:WC])
-
-    def scorer():
-        tc(R("pv0", 0, 28), R("pvf", 0, 28))
-        tc(R("uof", 0, 8), R("uoi", 0, 8))
-        quant("uq0", "us0", "ut", 0, 128)
-        run("v", [R("uq0", 0, 128), R("uof", 0, 8)], [R("uq", 0, 128)],
-            lambda: V.tensor_copy(T.uq[:, 0:128].bitcast(dt.uint32), T.uq0[:, 0:128].bitcast(dt.uint32).indirect(T.uof[:, 0:8])))
-        run("s", [R("us0", 0, 128), R("uof", 0, 8)], [R("us", 0, 128)],
-            lambda: g.scalar.activation(T.us[:, 0:128], T.us0[:, 0:128].indirect(T.uof[:, 0:8]), F_.Copy))
-        tc(R("pr16", 0, 84), R("pri", 0, 84))
-
-    def partners():
-        tc(R("prf", 0, 84), R("pri", 0, 84))
-        tt(R("pd", 0, 84), R("prf", 0, 84), R("jw", 0, 84), A_.subtract)
-        ts(R("col2", 0, 1), R("qcf", 0, 1), -2.0, 30.0, A_.mult, A_.add)
-
-    AB = ((0, G), (G, C))
-    HALVES = ((0, C // 2), (C // 2, C))
-
-    def windows(t, e):
-        return R("win0", 0, K) if t == 0 else R("win%d" % t, WC * e, WC * e + WC)
-
-    def offs(t, e, which, a, b):
-        a, b = a // 16, b // 16
-        if t == 0: return R("n4" if which == 0 else "p4", 28 * e + a, 28 * e + b)
-        o = 56 * (t - 1) + 28 * which
-        return R("l16", o + a, o + b)
-
-    def fetch(t, ch):
-        a, b = AB[ch]
-        for e in range(4): act(R("pb%d" % t, C * e + a, C * e + b), ind(windows(t, e), offs(t, e, 0, a, b)))
-
-    def addup(t, ch):
-        a, b = AB[ch]
-        for e in range(4): tt(R("z%d" % t, 4 * a + e, 4 * b, 4), ind(windows(t, e), offs(t, e, 1, a, b)), R("pb%d" % t, C * e + a, C * e + b), A_.add)
-        quant("zq%d" % t, "zs%d" % t, "z%d" % t, a, b)
-
-    def layer(t, ch):
-        a, b = AB[ch]
-        return [mm("wq", "wsc", 128 * k, "zq%d" % t, "zs%d" % t, a, b) for k in range(4)]
-
-    def score(t, ch):
-        a, b = AB[ch]
-        return mm("uq", "us", 0, "zq%d" % t, "zs%d" % t, a, b)
-
-    def relu(q, t, ch, k, o):
-        a, b = AB[ch]
-        out = R("h%d" % t, 4 * a + k, 4 * b, 4)
-        if q == "s": act(out, o, F_.Relu, scale=0.015625)
-        else: ts(out, o, 0.0, 0.015625, A_.max, A_.mult)
-
-    def unpack(t, src, a, b):
-        return [mm("eq", "es", 128 * k, ("gq%d" if src else "hq%d") % t, ("gs%d" if src else "hs%d") % t, a, b) for k in range(4)]
-
-    def keep(q, t, k, o, a):
-        copy(q, R("win%d" % (t + 1), WC * k + a, WC * k + a + o[2] - o[1]), o)
-
-    def send(t):
-        dst = T.cores[rank ^ (1 << t)]
-        rid, pid, _ = topo.addr(dst)
-        e = topo.engines(core, dst)[:8]
-        m = sum(1 << i for i in e)
-        h, s = "hq%d" % t, "hs%d" % t
-        order("g", [R(h, 0, G), R(s, 0, G)], [])
-        g.remote_dma(T["gq%d" % t][:, 0:G].bitcast(dt.uint8), T[h][:, 0:G].bitcast(dt.uint8), T.sem["arr%d" % t], T.sem.sent, pid, rid, m)
-        g.remote_dma(T["gs%d" % t][:, 0:G], T[s][:, 0:G], T.sem["arr%d" % t], T.sem.sent, pid, rid, m)
-        issued["sent"] = issued.get("sent", 0) + 2 * len(e)
-        tok = ("arr%d" % t, 2 * len(e))
-        issued[tok[0]] = tok[1]
-        note(tok, [], [R("gq%d" % t, 0, G), R("gs%d" % t, 0, G)])
-
-    for t in range(ROUNDS):
-        nr = "nxr%d" % (t + 1)
-        w = (28 * t, 28 * t + 28)
-        ssb, ssc, dif, sgn, scd, pvr = ["%s%d" % (n, t) for n in ("ssb", "ssc", "dif", "sgn", "scd", "pvr")]
-        fetch(t, 0)
-        addup(t, 0)
-        la = layer(t, 0)
-        if t: s0 = score(t, 0)
-        fetch(t, 1)
-        addup(t, 1)
-        if t: s1 = score(t, 1)
-        for k in range(4): relu(LA[k], t, 0, k, la[k])
-        quant("hq%d" % t, "hs%d" % t, "h%d" % t, 0, G)
-        send(t)
-        if t == 0:
-            scorer()
-            s0 = score(t, 0)
-            s1 = score(t, 1)
-            quant("eq", "es", "eo", 0, 512)
-        lb = layer(t, 1)
-        act(R(ssb, 0, G), s0)
-        tc(R(ssc, G, C), s1)
-        act(R(ssb, G, C), s1)
-        tc(R(ssc, 0, G), s0)
-        da = unpack(t, 0, 0, G)
-        for a, b in HALVES:
-            tt(R(dif, a, b), ind(R(ssb, 0, C), R("pr16", 28 * t + a // 16, 28 * t + b // 16)), R(ssc, a, b), A_.subtract)
-        if t == 0: partners()
-        for k in (0, 1): relu(LB[k], t, 1, k, lb[k])
-        for a, b in HALVES: act(R(sgn, a, b), R(dif, a, b), F_.Sign)
-        if t == 0:
-            act(R("sgp", 0, 84), R("pd", 0, 84), F_.Sign)
-            act(R("kap", 0, 84), R("sgp", 0, 84), F_.Identity, bias=R("col2", 0, 1))
-        for k in (2, 3): relu(LB[k], t, 1, k, lb[k])
-        for a, b in HALVES: scan(R(scd, a, b), R("db2", a, b), R(sgn, a, b), A_.add, A_.max)
-        tt(R("smf", 0, 28), R(scd, 15, C, 16), R("kap", *w), A_.is_equal)
-        tt(R("smm", 0, 28), R("smf", 0, 28), R("pd", *w), A_.mult)
-        tt(R("sms", 0, 28), R("smm", 0, 28), R("jw", 0, 28), A_.add)
-        tc(R("sig", 0, 28), R("sms", 0, 28))
-        quant("hq%d" % t, "hs%d" % t, "h%d" % t, G, C)
-        db = unpack(t, 0, G, C)
-        for k in range(4):
-            if DA[k] == "s": keep("s", t, k, da[k], 0)
-        act(R("sigr", 0, C), ind(R("iota", 0, C), R("sig", 0, 28)))
-        act(R(nr, 0, C), ind(R("nxr%d" % t, 0, C), R("sig", 0, 28)))
-        for k in range(4):
-            if DA[k] == "v": keep("v", t, k, da[k], 0)
-        for k in range(4):
-            if DB[k] == "v": keep("v", t, k, db[k], G)
-        pv = R("pv0", 0, 28) if t == 0 else R("l16", 56 * t - 28, 56 * t)
-        tc(R(pvr, 0, C), ind(R("sigr", 0, WC), pv))
-        scan(R("sb", 0, C), R("db", 0, C), R(nr, 0, C), A_.add, A_.max)
-        ts(R("l16", 56 * t, 56 * t + 28), R("sb", 15, C, 16), R("colb", 0, 1), None, A_.subtract)
-        for k in range(4):
-            if DB[k] == "s": keep("s", t, k, db[k], G)
-        scan(R("sb", C, 2 * C), R("db", 0, C), R(pvr, 0, C), A_.add, A_.max)
-        ts(R("l16", 56 * t + 28, 56 * t + 56), R("sb", C + 15, 2 * C, 16), R("colb", 0, 1), None, A_.subtract)
-        if t == 2: quant("vq", "vs", "vt", 0, 128)
-        dg = unpack(t, 1, 0, G)
-        for k in range(4): keep(DG[t][k], t, k, dg[k], C)
-    store("y", R("nxr3", 0, C), T.nl[:, 0:C], T.nxr3[0:128:16, 0:C])
-    fetch(3, 0)
-    addup(3, 0)
-    ya = mm("vq", "vs", 0, "zq3", "zs3", 0, G)
-    store("y", R("zq3", 0, G), T.oc[:, 0:4 * G], T.zq3[:, 0:G].bitcast(dt.uint8))
-    fetch(3, 1)
-    act(R("ysb", 0, G), ya)
-    store("y", R("ysb", 0, G), T.y[:, 0:G], T.ysb[:, 0:G])
-    addup(3, 1)
-    yb = mm("vq", "vs", 0, "zq3", "zs3", G, C)
-    for k in range(4): store("y", R("zs3", 0, C), T.osc[4 * k:4 * k + 4, 0:C], T.zs3[32 * k:32 * k + 4, 0:C])
-    store("s", R("zq3", G, C), T.oc[:, 4 * G:4 * C], T.zq3[:, G:C].bitcast(dt.uint8))
-    act(R("ysb", G, C), yb)
-    store("s", R("ysb", G, C), T.y[:, G:C], T.ysb[:, G:C])
     for s in sorted(issued):
         if waited.get(s, 0) < issued[s]: (g if s == "sent" else g.sync).wait_ge(T.sem[s], issued[s])

@@ -1,3 +1,4 @@
+import math
 from concourse.mybir import dt, AluOpType, ActivationFunctionType
 
 C, G, ROUNDS = 448, 256, 3
@@ -5,57 +6,33 @@ WC = C + G
 K = WC * 4
 UP = 1024.0
 F32, BF16, F16, I32, U16, U8, FP8 = "float32", "bfloat16", "float16", "int32", "uint16", "uint8", "float8_e4m3fn_x4"
-CFG = {
-    "read": [(0, 128, G, C)] * 3 + [(0, 128, 320, C)],
-    "layer": [(0, 128, G, C)] * 3, "send": [(0, 128, G), (0, G), (0, 128, G)],
-    "sr": [(0, 224, C)] * 3, "nr": [(0, C)] * 3, "pr": [(0, C)] * 4,
-    "score": [(0, G, C)] * 3, "pair": [(0, 224, C)] * 3, "bits": [(0, C)] * 3, "own": [(0, G, C)] * 3,
-}
+T1, T2, T3, T4, T5 = (0, C), (0, 128, C), (0, 128, G, C), (0, 128, 320, C), (0, 64, 128, G, C)
+CFG = {"f": [(0, 192, C), T5, T5, (0, 64, 128, 320, C)], "a": [T3, T5, (0, 64, 128, G, 352, C), (0, 64, 128, 320, C)],
+       "qz": [T3, T3, T3, T4], "r": [T3] * 3, "qh": [T3] * 3,
+       "send": [(0, 128, G), (0, G), (0, 128, G)], "sr": [T1] * 3, "score": [(0, G, C)] * 3, "sig": [T1] * 3, "sign": [T1] * 3,
+       "nx": [T2] * 3, "pv": [T1] + [T2] * 3, "pair": [(0, 224, C)] * 3, "own": [(0, G, C, WC)] * 3}
 ORDER = """
-Lnx:y Lx:y Lgh:y Lpr:y Lw:y Lws:y Lu:y ones:v Ip:g qh:v qq:v I16:g ql:v q:v I4:g Iu:g Ij:g qf:v uof:v na:v nb:v nc:s ca:v c4:s I84:g unit0:g unit1:g unit2:g unit3:g Ig:g c16:v q16:v nd:v c40:s d4:s nx16:v nxa:s d16:s n42:v jw:s f002:s n41:v inv:v n40:v n43:v f001:s f000:s p400s:v f003:s f013:s pd:v f011:s f012:s p400o:v f010:v f023:s f021:s a00:v f022:s hi:v qz00:v r001:s r002:s r000:s f020:s a01:v r003:v qz01:v qh00:v sc00:g qu:v r013:s r010:s a02:v uq:v r012:s cpd:s qz02:v us:s r011:s s00:s lo:v s01:s qh01:v sc01:g ss00:g lh:v r020:s lo01:s lo00:s Lv:y r022:s qe:v r023:s p0s0:v hi01:v hi00:v r021:s k002:s k001:s base:v b00:v p0o0:v sm0:v sa0:v sg0:v k003:s k000:s qh02:v nr00:s sr01:v k010:v k011:v sr00:s n10s:v k013:s k012:v g002:s n10o:v g001:s g000:v g003:s f10:s f11:s f12:s pr00:v p410s:v p410o:v a10:v a11:v qz10:v r101:s qz11:v r102:s a12:v r100:s r110:v qz12:v r103:s r111:s qh10:v r113:s r112:s qh11:v sc10:g ss10:g s10:s p1s0:v s11:s lo10:s r122:v lo11:v r120:s hi10:v r121:s r123:s k100:s hi11:v k102:s b10:v qh12:v sm1:v k101:s p1o0:v sa1:v k103:s k110:v k112:s sg1:v nr10:s k113:v sr11:v k111:s sr10:v g103:s n20s:v g102:v g101:s n20o:v g100:s f20:s f21:s f22:s pr10:v p420s:v p420o:v a20:v qz20:v r201:s r203:s a21:v r202:v r200:s qz21:v r210:s r212:s r213:s r211:s s20:s qh20:v sc20:g a22:v qh21:v sc21:g ss20:g k202:s qz22:v p2s0:v s21:v r222:s lo21:s lo20:v r220:v hi20:v hi21:v r221:s r223:s k203:s qh22:v b20:v p2o0:v sm2:v k200:s sa2:v k201:s k211:s sg2:v sr20:v k213:s k212:s sr21:s k210:v nr20:s Sna:y g201:s pr20:v g202:s n30s:v g200:v g203:s n30o:v p430s:v f30:s p430o:v f31:s qv:v a30:v qz30:v Sc0:y f32:s y0:s Sy0:y nxb:s Snb:y a31:v qz31:v Sc1:y a32:v y1:s Sy1:y qz32:v Sc2:y Ss0:s Ss1:y Ss2:s Ss3:y y2:v Sy2:y
+Lnx:y zero:v Ip:g Lx:y I4:g Lgh:y I16:g q:v Lpr:y ql:v qh:v q16:v qf:v Lw:y Lws:y Lu:y Ij:g I84:g na:s nb:s ones:v Lv:y i2:v k0:s Iu:g k1:v nm:s Ig:g jw:v i4:s nc:v uof:v ca:s c16:s unit:g c4:s nx16:v c40:s n41:v nd:v n42:v inv:v d4:s d16:s n40:v n43:v qe0:v f002:s ih:g p400s:v f001:s f003:v f000:s p400o:v f012:s qu:v hi:v a00:v f011:s f013:s f010:s uq:v qz00:v us:s qe3:v a01:v r002:s r001:s r003:s r000:s nxa:s qh00:v qz01:v a02:v sc00:g r012:s r011:s r010:s r013:s s00:s lo:v qz02:v lh:v qh01:v ul:v sc01:g s01:v r022:s ss00:g qe1:v pd:v lo00:s r023:v qe2:v lo01:s hi00:v r021:s r020:s hi01:v k003:s k000:s qh02:v k001:s b00:v k002:s p0s:v sm00:v k013:v k011:s p0o:v sg00:v k010:v k012:s nr00:v sr00:s nr01:v n10s:v k023:s k022:v nw0:g k020:s pr00:v n10o:v k021:s n11s:v p410s:v pr01:v f11:s n11o:v p410o:v f10:s p411s:v a11:v f12:s p411o:v a10:v f13:s a12:v qz10:v qz11:v a13:v r100:s r101:s r103:s r102:s r111:s r110:s r113:s r112:s s10:s qh10:v qz12:v p1s:v qh11:v s11:v sc10:g r120:v ss10:g r121:v lo11:s r123:v lo10:s hi11:v r122:s k103:s hi10:v k101:s k100:s qh12:v k102:s b10:v p1o:v sm10:v k111:v k110:s sg10:v k112:s k113:v sr10:s nr10:v nr11:v k120:s n20s:v pr10:v k121:s nw1:g k123:v k122:s n20o:v p420s:v pr11:v f20:s n21s:v p420o:v f21:s p421s:v n21o:v a20:v f22:s a21:v f23:s p421o:v qz20:v a22:v r200:s r203:s r201:s r202:s p2s:v qz21:v a23:v r211:s r212:s r213:s qh20:v r210:s a24:v nxb:s sc20:g s20:s Snb:y qh21:v qz22:v ss20:g qv:v sc21:g p2o:v k202:s s21:v lo21:s lo20:v r220:s hi21:v r223:s r222:s r221:s hi20:v k203:s k201:s qh22:v k200:s b20:v sm20:v k211:s k210:v k213:s sg20:v sr20:s k212:v nr20:v k223:s nr21:v n30s:v pr20:v n30o:v k222:s nw2:g pr21:v n31s:v k220:s p430s:v k221:s p431s:v n31o:v p430o:v f31:v f30:s Sna:y p431o:v f32:s a30:v a31:v f33:s a32:v qz30:v qz31:v Sc0:y a33:v y0:s Sy0:y y1:s Sc1:y Sy1:y qz32:v Sc2:y Ss0:s y2:v Ss2:y Ss1:s Sy2:y Ss3:s
 """
 
-SCRATCH = {
-    "nxi": ("sbuf", [128, 44], I32), "pri": ("sbuf", [128, 84], I32), "nx16": ("sbuf", [128, 44], U16),
-    "n4": ("sbuf", [128, 112], U16),
-    "wq": ("sbuf", [128, 512], FP8), "wsc": ("sbuf", [128, 512], U8),
-    "ut": ("sbuf", [128, 512], BF16), "uq0": ("sbuf", [128, 128], FP8), "us0": ("sbuf", [128, 128], U8),
-    "uq": ("sbuf", [128, 128], FP8), "us": ("sbuf", [128, 128], U8), "uof": ("sbuf", [128, 8], U16),
-    "vt": ("sbuf", [128, 512], BF16), "vq": ("sbuf", [128, 128], FP8), "vs": ("sbuf", [128, 128], U8),
-    "et": ("sbuf", [128, 512], BF16), "eo": ("sbuf", [128, 2048], BF16),
-    "eq": ("sbuf", [128, 512], FP8), "es": ("sbuf", [128, 512], U8),
-    "pci": ("sbuf", [128, 28], I32), "qci": ("sbuf", [128, 32], I32), "q16": ("sbuf", [128, 28], U16),
-    "col": ("sbuf", [128, 16], F32), "nar": ("sbuf", [128, 192], F32),
-    "d16": ("sbuf", [128, C], BF16), "d4": ("sbuf", [128, C], BF16),
-    "uoi": ("sbuf", [128, 8], I32), "i84": ("sbuf", [128, 84], F32), "jw": ("sbuf", [128, 84], F32),
-    "lohi": ("sbuf", [128, 168], F32), "lh16": ("sbuf", [128, 168], U16),
-    "pd": ("sbuf", [128, 84], F32), "cpd": ("sbuf", [128, 84], F32), "base": ("sbuf", [128, 84], F32),
-    "iota": ("sbuf", [128, WC], F32), "inv": ("sbuf", [128, WC], F32), "nxr0": ("sbuf", [128, WC], F32),
-    "sigr": ("sbuf", [128, WC], F32),
-    "sm": ("sbuf", [128, 56 * 3], F32), "sig": ("sbuf", [128, 84], U16),
-    "ysb": ("sbuf", [128, C], F32), "ps": ("psum", [128, 4096], F32),
-}
+SCRATCH = {"ps": ("psum", [128, 4096], F32)}
+for _n, _w, _d in (("nxi", 44, I32), ("pri", 84, I32), ("nx16", 44, U16), ("n4", 112, U16), ("wq", 512, FP8), ("wsc", 512, U8),
+                   ("ut", 512, BF16), ("uq0", 128, FP8), ("us0", 128, U8), ("uq", 128, FP8), ("us", 128, U8), ("uof", 8, U16),
+                   ("vt", 512, BF16), ("vq", 128, FP8), ("vs", 128, U8), ("et", 128, BF16), ("eo", 516, BF16), ("eq", 512, FP8), ("es", 512, U8),
+                   ("pci", 28, I32), ("qci", 32, I32), ("q16", 28, U16), ("col", 16, F32), ("nar", 240, F32),
+                   ("d16", C, BF16), ("d4", C, BF16), ("uoi", 8, I32), ("i84", 84, F32),
+                   ("iota", WC, F32), ("inv", WC, F32), ("nxr0", WC, F32), ("invh", C, F16), ("sigr", WC, F32),
+                   ("sm", 252, F32), ("k3", 252, F32), ("scd", 9 * C + 32, F16), ("lohi", 168, F32), ("lh16", 168, U16),
+                   ("sig", 84, U16), ("sb", 2 * C, F32), ("ysb", C, F32)):
+    SCRATCH[_n] = ("sbuf", [128, _w], _d)
 for _t in range(4):
-    SCRATCH["win%d" % _t] = ("sbuf", [128, K], BF16)
-    SCRATCH["pb%d" % _t] = ("sbuf", [128, 4 * C], BF16)
-    SCRATCH["z%d" % _t] = ("sbuf", [128, 4 * C], BF16)
-    SCRATCH["zq%d" % _t] = ("sbuf", [128, C], FP8)
-    SCRATCH["zs%d" % _t] = ("sbuf", [128, C], U8)
-    SCRATCH["sb%d" % _t] = ("sbuf", [128, 3 * C], F32)
-    SCRATCH["sh%d" % _t] = ("sbuf", [128, 3 * C], F16)
-    SCRATCH["l%d" % _t] = ("sbuf", [128, 252], U16)
+    for _n, _w, _d in (("win", K, BF16), ("pb", 4 * C, BF16), ("z", 4 * C, BF16), ("zq", C, FP8), ("zs", C, U8), ("sh", 3 * C, F16), ("l", 252, U16)):
+        SCRATCH[_n + str(_t)] = ("sbuf", [128, _w], _d)
 for _t in range(3):
-    SCRATCH["h%d" % _t] = ("sbuf", [128, 4 * C], BF16)
-    SCRATCH["hq%d" % _t] = ("sbuf", [128, C], FP8)
-    SCRATCH["hs%d" % _t] = ("sbuf", [128, C], U8)
-    SCRATCH["gq%d" % _t] = ("sbuf", [128, G], FP8)
-    SCRATCH["gs%d" % _t] = ("sbuf", [128, G], U8)
+    for _n, _w, _d in (("h", 4 * C, BF16), ("hq", WC, FP8), ("hs", WC, U8), ("pvr", C, F16), ("ssb", C, F32), ("ssc", C, F32),
+                       ("nxh", C, F16), ("cmp", C, BF16)):
+        SCRATCH[_n + str(_t)] = ("sbuf", [128, _w], _d)
     SCRATCH["nxr%d" % (_t + 1)] = ("sbuf", [128, C], F32)
-    SCRATCH["pvr%d" % _t] = ("sbuf", [128, C], F16)
-    SCRATCH["ssb%d" % _t] = ("sbuf", [128, C], F32)
-    SCRATCH["slo%d" % _t] = ("sbuf", [128, C], F32)
-    SCRATCH["bit%d" % _t] = ("sbuf", [128, C], BF16)
-    SCRATCH["scd%d" % _t] = ("sbuf", [128, C], F16)
 
 SEMAPHORES = ["cv", "cs", "cp", "cg", "sent", "st"] + ["ld%d" % i for i in range(8)] + ["arr%d" % t for t in range(3)]
 
@@ -98,12 +75,14 @@ def calls(g, core, T, topo, bank):
 
     def tc(n, out, a): op(n, "v", flat([a]), [out], lambda q: V.tensor_copy(ap(out), ap(a)))
 
+    def fill(n, out, c): op(n, "v", [], [out], lambda q: V.memset(ap(out), c))
+
     def ts(n, out, a, s1, s2, o0, o1=None):
         if o1 is None: op(n, "v", flat([a, s1]), [out], lambda q: V.tensor_scalar(ap(out), ap(a), val(s1), None, o0))
         else: op(n, "v", flat([a, s1, s2]), [out], lambda q: V.tensor_scalar(ap(out), ap(a), val(s1), val(s2), o0, o1))
 
-    def scan(n, out, d0, d1):
-        op(n, "v", [d0, d1], [out], lambda q: V.tensor_tensor_scan(ap(out), ap(d0), ap(d1), 0.0, A_.add, A_.max))
+    def scan(n, out, d0, d1, o0=A_.add, o1=A_.max):
+        op(n, "v", [d0, d1], [out], lambda q: V.tensor_tensor_scan(ap(out), ap(d0), ap(d1), 0.0, o0, o1))
 
     def copy(n, qs, out, a):
         op(n, qs, flat([a]), [out], lambda q: S.activation(ap(out), ap(a), F_.Copy) if q == "s" else V.tensor_copy(ap(out), ap(a)))
@@ -113,12 +92,15 @@ def calls(g, core, T, topo, bank):
         op(n, qs, flat([a, add]), [out], lambda q: S.activation(ap(out), ap(a), fn, bias=val(add), scale=mul) if q == "s"
            else V.tensor_scalar(ap(out), ap(a), mul, val(add), A_.mult, A_.add))
 
+    def act(n, out, a, fn, mul, add):
+        op(n, "s", flat([a, add]), [out], lambda q: S.activation(ap(out), ap(a), fn, bias=val(add), scale=mul))
+
     def relu(n, out, a):
         op(n, "sv", [a], [out], lambda q: S.activation(ap(out), ap(a), F_.Relu, scale=0.015625) if q == "s"
            else V.tensor_scalar(ap(out), ap(a), 0.0, 0.015625, A_.max, A_.mult))
 
-    def quant(n, q, s, t, a, b):
-        op(n, "v", [R(t, 4 * a, 4 * b)], [R(q, a, b), R(s, a, b)], lambda _: V.quantize_mx(T[q][:, a:b], T[s][:, a:b], T[t][:, 4 * a:4 * b]))
+    def quant(n, q, s, a, b, src):
+        op(n, "v", [src], [R(q, a, b), R(s, a, b)], lambda _: V.quantize_mx(T[q][:, a:b], T[s][:, a:b], ap(src)))
 
     def mm(n, wq, ws, wa, xq, xs, a, b):
         o = ("ps", n, b - a, 1)
@@ -131,10 +113,13 @@ def calls(g, core, T, topo, bank):
         if SCRATCH[name][2] == F32: op(n, "g", [], [o], lambda q: g.iota(ap(o), pattern, base, cm, allow_small_or_imprecise_dtypes=True))
         else: op(n, "g", [], [o], lambda q: g.iota(ap(o), pattern, base, cm))
 
+    def gcopy(n, out, a):
+        op(n, "g", [a], [out], lambda q: g.affine_select(ap(out), ap(a), [[0, a[2] - a[1]]], A_.is_ge, 0.0, 0, 0))
+
     nld = [0]
 
     def load(n, r, dst, src):
-        op(n, "ys", [], [r], lambda q: dq[q].dma_start(dst, src), "ld%d" % nld[0])
+        op(n, "y", [], [r], lambda q: dq[q].dma_start(dst, src), "ld%d" % nld[0])
         nld[0] += 1
 
     def store(n, r, dst, src):
@@ -154,125 +139,129 @@ def calls(g, core, T, topo, bank):
     iota("Ip", "pci", 0, 28, [[0, 28]], 0, 1)
     iota("I16", "nar", 7, 32, [[1, 25]], -1, 0)
     iota("I4", "nar", 32, 48, [[0, 4], [1, 4]], 0, 0)
-    iota("Ij", "iota", 0, WC, [[1, WC]], 0, 0)
+    iota("Ij", "iota", 0, WC // 4, [[1, WC // 4]], 0, 0)
+    affine("i2", "sv", R("iota", WC // 4, WC // 2), R("iota", 0, WC // 4), 1.0, float(WC // 4))
+    affine("i4", "sv", R("iota", WC // 2, WC), R("iota", 0, WC // 2), 1.0, float(WC // 2))
     iota("Iu", "uoi", 0, 8, [[16, 8]], 0, 0)
     iota("I84", "i84", 0, 84, [[0, 3], [16, 28]], 0, 0)
-    op("ones", "v", [], [R("et", 0, 512)], lambda q: V.memset(T.et[:], 1.0))
-    for b in range(4):
-        op("unit%d" % b, "g", [R("et", 0, 512)], [R("eo", 512 * b, 512 * b + 512)],
-           lambda q, b=b: g.affine_select(T.eo[:, 512 * b:512 * b + 512], T.et[:], [[1, 512]], A_.is_equal, 0.0, -b, -4))
+    fill("ones", R("et", 0, 128), 1.0)
+    fill("zero", R("eo", 0, 516), 0.0)
+    op("unit", "g", [R("et", 0, 128)], [R("eo", 3, 515, 4)],
+       lambda q: g.affine_select(T.eo[:, 3:515:4], T.et[:], [[1, 128]], A_.is_equal, 0.0, 0, -1))
+    for b in range(4): quant("qe%d" % b, "eq", "es", 128 * b, 128 * b + 128, R("eo", 3 - b, 515 - b))
     iota("Ig", "sigr", C, WC, [[1, G]], C, 0)
+    affine("k0", "sv", R("k3", 0, 252, 3), R("iota", 0, 84), 0.0, 0.0)
+    affine("k1", "sv", R("k3", 1, 252, 3), R("iota", 0, 84), 0.0, 1.0)
     ts("q", R("qci", 0, 28), R("pci", 0, 28), 15, None, A_.bitwise_and)
-    ts("qh", R("qci", 29, 30), R("pci", 0, 1), 2, 3, A_.arith_shift_right, A_.bitwise_and)
-    ts("ql", R("qci", 30, 31), R("pci", 0, 1), 3, None, A_.bitwise_and)
-    ts("qq", R("qci", 28, 29), R("pci", 0, 1), 15, None, A_.bitwise_and)
-    tc("qf", R("col", 0, 3), R("qci", 28, 31))
+    ts("qh", R("qci", 28, 29), R("pci", 0, 1), 2, 3, A_.arith_shift_right, A_.bitwise_and)
+    ts("ql", R("qci", 29, 30), R("pci", 0, 1), 3, None, A_.bitwise_and)
+    tc("qf", R("col", 0, 3), R("qci", 27, 30))
     tc("q16", R("q16", 0, 28), R("qci", 0, 28))
-    ts("na", R("nar", 55, 80), R("nar", 7, 32), Q, -4.0 * UP, A_.is_equal, A_.mult)
-    ts("nb", R("nar", 80, 96), R("nar", 32, 48), QH, -4.0 * UP, A_.is_equal, A_.mult)
-    affine("nc", "sv", R("nar", 104, 144), R("nar", 55, 95), -0.25, 0.0)
-    tt("nd", R("nar", 152, 192), R("nar", 56, 96), R("nar", 104, 144), A_.add)
+    act("na", R("nar", 55, 80), R("nar", 7, 32), F_.Abs, -1.0, Q)
+    act("nb", R("nar", 80, 96), R("nar", 32, 48), F_.Abs, -1.0, QH)
+    act("nm", R("nar", 104, 145), R("nar", 55, 96), F_.Relu, -UP, UP)
+    affine("nc", "sv", R("nar", 200, 240), R("nar", 105, 145), -4.0, 0.0)
+    tt("nd", R("nar", 152, 192), R("nar", 200, 240), R("nar", 104, 144), A_.add)
     copy("d4", "s", R("d4", 0, C), ind(R("nar", 176, 192), R("q16", 0, 28)))
     copy("d16", "s", R("d16", 0, C), ind(R("nar", 152, 168), R("q16", 0, 28)))
-    ts("c16", C16, Q, 15.0, UP, A_.is_lt, A_.mult)
-    ts("ca", CA, QH, 3.0, UP, A_.is_lt, A_.mult)
+    affine("c16", "sv", C16, R("nar", 120, 121), -1.0, UP)
+    affine("ca", "sv", CA, R("nar", 132, 133), -1.0, UP)
     affine("c4", "sv", C4, QL, -float(WC), CA)
     affine("c40", "sv", C40, QL, -0.25, CA)
-    affine("jw", "sv", R("jw", 0, 84), R("i84", 0, 84), 1.0, Q)
+    PD, JW = R("k3", 2, 252, 3), R("scd", 77, 77 + 48 * 83 + 1, 48)
+    ts("jw", JW, R("i84", 0, 84), Q, None, A_.add)
+    ts("ul", R("scd", 61, 61 + 48 * 83 + 1, 48), R("i84", 0, 84), 0.0, C16, A_.mult, A_.subtract)
 
     def four(n, t, k, row, a, b):
-        sb = "sh%d" % t if t and k else "sb%d" % t
+        sb = "sh%d" % t if t else "sb"
         scan(n + "s", R(sb, C * k + a, C * k + b), R("d4", a, b), R(row, a, b))
         o, s = R("l%d" % t, 112 * k + a // 4, 112 * k + b // 4), R(sb, C * k + a + 3, C * k + b, 4)
         if t == 0: ts(n + "o", o, s, C40, 4.0, A_.subtract, A_.mult)
         else: ts(n + "o", o, s, C4, None, A_.subtract)
 
     def previous(t, row):
-        for i, (a, b) in enumerate(cuts(CFG["pr"][t])): four("p4%d%d" % (t, i), t, 1, row, a, b)
+        for i, (a, b) in enumerate(cuts(CFG["pv"][t])): four("p4%d%d" % (t, i), t, 1, row, a, b)
         if t < ROUNDS:
-            sb = "sh%d" % t if t else "sb%d" % t
-            scan("p%ds0" % t, R(sb, 2 * C, 3 * C), R("d16", 0, C), R(row, 0, C))
-            ts("p%do0" % t, R("l%d" % t, 224, 252), R(sb, 2 * C + 15, 3 * C, 16), C16, None, A_.subtract)
+            sb = "sh%d" % t
+            scan("p%ds" % t, R(sb, 2 * C, 3 * C), R("d16", 0, C), R(row if t else "invh", 0, C))
+            ts("p%do" % t, R("l%d" % t, 224, 252), R(sb, 2 * C + 15, 3 * C, 16), C16, None, A_.subtract)
 
     tc("nx16", R("nx16", 0, 44), R("nxi", 0, 44))
     for e in range(4): ts("n4%d" % e, R("n4", 28 * e, 28 * e + 28), R("nxi", 0, 28), 4.0, float(e), A_.mult, A_.add)
     op("inv", "v", [R("nx16", 0, 44), R("iota", 0, WC)], [R("inv", 0, WC)],
        lambda q: V.tensor_copy(T.inv[:, 0:WC].indirect(T.nx16[:, 0:44]), T.iota[:, 0:WC]))
+    gcopy("ih", R("invh", 0, C), R("inv", 0, C))
     previous(0, "inv")
     copy("nxa", "sv", R("nxr0", 0, C), ind(R("iota", 0, WC), R("nx16", 0, 28)))
     copy("nxb", "sv", R("nxr0", C, WC), ind(R("iota", 0, WC), R("nx16", 28, 44)))
     store("Snb", R("nxr0", C, WC), T.nl[:, C:WC], T.nxr0[0:128:16, C:WC])
     tc("uof", R("uof", 0, 8), R("uoi", 0, 8))
-    quant("qu", "uq0", "us0", "ut", 0, 128)
+    quant("qu", "uq0", "us0", 0, 128, R("ut", 0, 512))
     op("uq", "v", [R("uq0", 0, 128), R("uof", 0, 8)], [R("uq", 0, 128)],
        lambda q: V.tensor_copy(T.uq[:, 0:128].bitcast(dt.uint32), T.uq0[:, 0:128].bitcast(dt.uint32).indirect(T.uof[:, 0:8])))
     copy("us", "sv", R("us", 0, 128), ind(R("us0", 0, 128), R("uof", 0, 8)))
-    quant("qe", "eq", "es", "eo", 0, 512)
-    quant("qv", "vq", "vs", "vt", 0, 128)
-    tt("lo", R("lohi", 0, 84), R("pri", 0, 84), R("jw", 0, 84), A_.min)
-    tt("hi", R("lohi", 84, 168), R("pri", 0, 84), R("jw", 0, 84), A_.max)
+    quant("qv", "vq", "vs", 0, 128, R("vt", 0, 512))
+    tt("lo", R("lohi", 0, 84), R("pri", 0, 84), JW, A_.min)
+    tt("hi", R("lohi", 84, 168), R("pri", 0, 84), JW, A_.max)
     tc("lh", R("lh16", 0, 168), R("lohi", 0, 168))
-    tt("pd", R("pd", 0, 84), R("pri", 0, 84), R("jw", 0, 84), A_.subtract)
-    op("cpd", "sv", [R("pd", 0, 84), C16], [R("cpd", 0, 84)], lambda q: S.activation(T.cpd[:], T.pd[:], F_.Identity, scale=ap(C16)) if q == "s"
-       else V.tensor_scalar(T.cpd[:], T.pd[:], ap(C16), None, A_.mult))
-    tt("base", R("base", 0, 84), R("jw", 0, 84), R("cpd", 0, 84), A_.subtract)
+    tt("pd", PD, R("pri", 0, 84), JW, A_.subtract)
 
     def reading(t):
         w, l, pb, z = R("win%d" % t, 0, K), "l%d" % t, "pb%d" % t, "z%d" % t
-        for i, (a, b) in enumerate(cuts(CFG["read"][t])):
+        for i, (a, b) in enumerate(cuts(CFG["f"][t])):
             n = "%d%d" % (t, i)
             if t == 0:
                 for e in range(4): copy("f%s%d" % (n, e), "sv", R(pb, 4 * a + e, 4 * b, 4), ind(w, R("n4", 28 * e + a // 16, 28 * e + b // 16)))
             else: copy("f" + n, "sv", R(pb, 4 * a, 4 * b), ind(w, R(l, a // 4, b // 4)))
-            tt("a" + n, R(z, 4 * a, 4 * b), ind(w, R(l, 112 + a // 4, 112 + b // 4)), R(pb, 4 * a, 4 * b), A_.add)
+        for i, (a, b) in enumerate(cuts(CFG["a"][t])):
+            tt("a%d%d" % (t, i), R(z, 4 * a, 4 * b), ind(w, R(l, 112 + a // 4, 112 + b // 4)), R(pb, 4 * a, 4 * b), A_.add)
+        for i, (a, b) in enumerate(cuts(CFG["qz"][t])): quant("qz%d%d" % (t, i), "zq%d" % t, "zs%d" % t, a, b, R(z, 4 * a, 4 * b))
 
     def send(t):
         dst = T.cores[rank ^ (1 << t)]
         rid, pid, _ = topo.addr(dst)
-        e = topo.engines(core, dst)[:8]
-        m, pieces = sum(1 << i for i in e), cuts(CFG["send"][t])
-        h, s, gq, gs, arr = "hq%d" % t, "hs%d" % t, "gq%d" % t, "gs%d" % t, "arr%d" % t
+        e, m, pieces = topo.engines(core, dst), topo.mask(core, dst), cuts(CFG["send"][t])
+        h, s, arr = "hq%d" % t, "hs%d" % t, "arr%d" % t
         sem = (arr, len(e), len(e) * (len(pieces) + 1))
         for i, (a, b) in enumerate(pieces):
-            op("sc%d%d" % (t, i), "g", [R(h, a, b)], [R(gq, a, b)], lambda q, a=a, b=b: g.remote_dma(
-                T[gq][:, a:b].bitcast(dt.uint8), T[h][:, a:b].bitcast(dt.uint8), T.sem[arr], T.sem.sent, pid, rid, m), sem)
-        op("ss%d0" % t, "g", [R(s, 0, G)], [R(gs, 0, G)], lambda q: g.remote_dma(T[gs][:, 0:G], T[s][:, 0:G], T.sem[arr], T.sem.sent, pid, rid, m), sem)
+            op("sc%d%d" % (t, i), "g", [R(h, a, b)], [R(h, C + a, C + b)], lambda q, a=a, b=b: g.remote_dma(
+                T[h][:, C + a:C + b].bitcast(dt.uint8), T[h][:, a:b].bitcast(dt.uint8), T.sem[arr], T.sem.sent, pid, rid, m), sem)
+        op("ss%d0" % t, "g", [R(s, 0, G)], [R(s, C, WC)], lambda q: g.remote_dma(T[s][:, C:WC], T[s][:, 0:G], T.sem[arr], T.sem.sent, pid, rid, m), sem)
 
     for t in range(ROUNDS):
         zq, zs, h, hq, hs, win = "zq%d" % t, "zs%d" % t, "h%d" % t, "hq%d" % t, "hs%d" % t, "win%d" % (t + 1)
-        ssb, slo, bit, scd, pvr, nr = "ssb%d" % t, "slo%d" % t, "bit%d" % t, "scd%d" % t, "pvr%d" % t, "nxr%d" % (t + 1)
+        ssb, ssc, cmp, pvr, nr, nh = "ssb%d" % t, "ssc%d" % t, "cmp%d" % t, "pvr%d" % t, "nxr%d" % (t + 1), "nxh%d" % t
         reading(t)
-        for i, (a, b) in enumerate(cuts(CFG["layer"][t])):
-            n = "%d%d" % (t, i)
-            quant("qz" + n, zq, zs, "z%d" % t, a, b)
-            for k in range(4): relu("r%s%d" % (n, k), R(h, 4 * a + k, 4 * b, 4), mm("mw%s%d" % (n, k), "wq", "wsc", 128 * k, zq, zs, a, b))
-            quant("qh" + n, hq, hs, h, a, b)
+        for i, (a, b) in enumerate(cuts(CFG["r"][t])):
+            for k in range(4): relu("r%d%d%d" % (t, i, k), R(h, 4 * a + k, 4 * b, 4), mm("mw%d%d%d" % (t, i, k), "wq", "wsc", 128 * k, zq, zs, a, b))
+        for i, (a, b) in enumerate(cuts(CFG["qh"][t])): quant("qh%d%d" % (t, i), hq, hs, a, b, R(h, 4 * a, 4 * b))
         send(t)
         for i, (a, b) in enumerate(cuts(CFG["score"][t])): copy("s%d%d" % (t, i), "sv", R(ssb, a, b), mm("mu%d%d" % (t, i), "uq", "us", 0, zq, zs, a, b))
         for i, (a, b) in enumerate(cuts(CFG["pair"][t])):
             o = 28 * t + a // 16, 28 * t + b // 16
-            copy("lo%d%d" % (t, i), "sv", R(slo, a, b), ind(R(ssb, 0, C), R("lh16", *o)))
-            tt("hi%d%d" % (t, i), R(bit, a, b), ind(R(ssb, 0, C), R("lh16", 84 + o[0], 84 + o[1])), R(slo, a, b), A_.is_gt)
-        for i, (a, b) in enumerate(cuts(CFG["bits"][t])): scan("b%d%d" % (t, i), R(scd, a, b), R("d16", a, b), R(bit, a, b))
-        w = (28 * t, 28 * t + 28)
-        tt("sm%d" % t, R("sm", 56 * t, 56 * t + 28), R(scd, 15, C, 16), R("pd", *w), A_.mult)
-        tt("sa%d" % t, R("sm", 56 * t + 28, 56 * t + 56), R("sm", 56 * t, 56 * t + 28), R("base", *w), A_.add)
-        tc("sg%d" % t, R("sig", *w), R("sm", 56 * t + 28, 56 * t + 56))
+            copy("lo%d%d" % (t, i), "sv", R(ssc, a, b), ind(R(ssb, 0, C), R("lh16", *o)))
+            tt("hi%d%d" % (t, i), R(cmp, a, b), ind(R(ssb, 0, C), R("lh16", 84 + o[0], 84 + o[1])), R(ssc, a, b), A_.is_gt)
+        for i, (a, b) in enumerate(cuts(CFG["sign"][t])):
+            a3, b3 = 3 * (C * t + a), 3 * (C * t + b)
+            scan("b%d%d" % (t, i), R("scd", a3, b3 - 2, 3), R("d16", a, b), R(cmp, a, b))
+        for i, (a, b) in enumerate(cuts(CFG["sig"][t])):
+            a3, b3 = 3 * (C * t + a), 3 * (C * t + b)
+            scan("sm%d%d" % (t, i), R("sm", a3 // 16, b3 // 16), R("k3", a3 // 16, b3 // 16), R("scd", a3 + 45, b3 + 30, 16), A_.mult, A_.add)
+            tc("sg%d%d" % (t, i), R("sig", a3 // 48, b3 // 48), R("sm", a3 // 16 + 2, b3 // 16, 3))
         for i, (a, b) in enumerate(cuts(CFG["sr"][t])):
             copy("sr%d%d" % (t, i), "sv", R("sigr", a, b), ind(R("iota", 0, C), R("sig", 28 * t + a // 16, 28 * t + b // 16)))
-        for i, (a, b) in enumerate(cuts(CFG["nr"][t])):
-            copy("nr%d%d" % (t, i), "sv", R(nr, a, b), ind(R("nxr%d" % t, 0, C), R("sig", 28 * t + a // 16, 28 * t + b // 16)))
-            four("n%d%d" % (t + 1, i), t + 1, 0, nr, a, b)
-        for i, (a, b) in enumerate(cuts(CFG["pr"][t + 1])):
+        for i, (a, b) in enumerate(cuts(CFG["nx"][t])):
+            copy("nr%d%d" % (t, i), "v", R(nh, a, b), ind(R("nxr%d" % t, 0, C), R("sig", 28 * t + a // 16, 28 * t + b // 16)))
+            four("n%d%d" % (t + 1, i), t + 1, 0, nh, a, b)
+        gcopy("nw%d" % t, R(nr, 0, C), R(nh, 0, C))
+        for i, (a, b) in enumerate(cuts(CFG["pv"][t + 1])):
             copy("pr%d%d" % (t, i), "v", R(pvr, a, b), ind(R("sigr", 0, WC), R("l%d" % t, 224 + a // 16, 224 + b // 16)))
         previous(t + 1, pvr)
         for i, (a, b) in enumerate(cuts(CFG["own"][t])):
             for k in range(4): copy("k%d%d%d" % (t, i, k), "sv", R(win, WC * k + a, WC * k + b), mm("me%d%d%d" % (t, i, k), "eq", "es", 128 * k, hq, hs, a, b))
-        for k in range(4): copy("g%d0%d" % (t, k), "sv", R(win, WC * k + C, WC * k + WC), mm("mg%d0%d" % (t, k), "eq", "es", 128 * k, "gq%d" % t, "gs%d" % t, 0, G))
     store("Sna", R("nxr3", 0, C), T.nl[:, 0:C], T.nxr3[0:128:16, 0:C])
     reading(3)
-    for i, (a, b) in enumerate(cuts(CFG["read"][3])):
-        quant("qz3%d" % i, "zq3", "zs3", "z3", a, b)
+    for i, (a, b) in enumerate(cuts(CFG["qz"][3])):
         store("Sc%d" % i, R("zq3", a, b), T.oc[:, 4 * a:4 * b], T.zq3[:, a:b].bitcast(dt.uint8))
         copy("y%d" % i, "sv", R("ysb", a, b), mm("mv%d" % i, "vq", "vs", 0, "zq3", "zs3", a, b))
         store("Sy%d" % i, R("ysb", a, b), T.y[:, a:b], T.ysb[:, a:b])
@@ -282,7 +271,7 @@ def calls(g, core, T, topo, bank):
 
 def clash(a, lo, hi, step):
     if a[1] <= lo or hi <= a[0]: return False
-    return not (a[2] == step and step > 1 and (a[0] - lo) % step)
+    return (a[0] - lo) % math.gcd(a[2], step) == 0
 
 
 def rank_program(g, core, T, topo):
@@ -294,7 +283,7 @@ def rank_program(g, core, T, topo):
     seq = []
     for w in ORDER.split():
         name, q = w.split(":")
-        if q != "p": seq += [(by[r[1]], "p") for r in by[name][2] if r[0] == "ps"] + [(by[name], q)]
+        seq += [(by[r[1]], "p") for r in by[name][2] if r[0] == "ps"] + [(by[name], q)]
     assert len(seq) == len(ops) == len({o[0][0] for o in seq})
     eng = {"v": g.vector, "s": g.scalar, "p": g.tensor, "g": g, "y": g.sync}
     csem = {"v": "cv", "s": "cs", "p": "cp", "g": "cg"}

import math
from concourse.mybir import dt, AluOpType, ActivationFunctionType

C, G, ROUNDS = 448, 256, 3
WC = C + G
K = WC * 4
UP = 1024.0
F32, BF16, F16, I32, U16, U8, FP8 = "float32", "bfloat16", "float16", "int32", "uint16", "uint8", "float8_e4m3fn_x4"
T1, T2, T3, T4, T5 = (0, C), (0, 128, C), (0, 128, G, C), (0, 128, 320, C), (0, 64, 128, G, C)
CFG = {"f": [(0, 192, C), T5, T5, (0, 64, 128, 320, C)], "a": [T3, T5, (0, 64, 128, G, 352, C), (0, 64, 128, 320, C)],
       "qz": [T3, T3, T3, T4], "r": [T3] * 3, "qh": [T3] * 3,
       "send": [(0, 128, G), (0, G), (0, 128, G)], "sr": [T1] * 3, "score": [(0, G, C)] * 3, "sig": [T1] * 3, "sign": [T1] * 3,
       "nx": [T2] * 3, "pv": [T1] + [T2] * 3, "pair": [(0, 224, C)] * 3, "own": [(0, G, C, WC)] * 3}
ORDER = """
Lnx:y zero:v Ip:g Lx:y I4:g Lgh:y I16:g q:v Lpr:y ql:v qh:v q16:v qf:v Lw:y Lws:y Lu:y Ij:g I84:g na:s nb:s ones:v Lv:y i2:v k0:s Iu:g k1:v nm:s Ig:g jw:v i4:s nc:v uof:v ca:s c16:s unit:g c4:s nx16:v c40:s n41:v nd:v n42:v inv:v d4:s d16:s n40:v n43:v qe0:v f002:s ih:g p400s:v f001:s f003:v f000:s p400o:v f012:s qu:v hi:v a00:v f011:s f013:s f010:s uq:v qz00:v us:s qe3:v a01:v r002:s r001:s r003:s r000:s nxa:s qh00:v qz01:v a02:v sc00:g r012:s r011:s r010:s r013:s s00:s lo:v qz02:v lh:v qh01:v ul:v sc01:g s01:v r022:s ss00:g qe1:v pd:v lo00:s r023:v qe2:v lo01:s hi00:v r021:s r020:s hi01:v k003:s k000:s qh02:v k001:s b00:v k002:s p0s:v sm00:v k013:v k011:s p0o:v sg00:v k010:v k012:s nr00:v sr00:s nr01:v n10s:v k023:s k022:v nw0:g k020:s pr00:v n10o:v k021:s n11s:v p410s:v pr01:v f11:s n11o:v p410o:v f10:s p411s:v a11:v f12:s p411o:v a10:v f13:s a12:v qz10:v qz11:v a13:v r100:s r101:s r103:s r102:s r111:s r110:s r113:s r112:s s10:s qh10:v qz12:v p1s:v qh11:v s11:v sc10:g r120:v ss10:g r121:v lo11:s r123:v lo10:s hi11:v r122:s k103:s hi10:v k101:s k100:s qh12:v k102:s b10:v p1o:v sm10:v k111:v k110:s sg10:v k112:s k113:v sr10:s nr10:v nr11:v k120:s n20s:v pr10:v k121:s nw1:g k123:v k122:s n20o:v p420s:v pr11:v f20:s n21s:v p420o:v f21:s p421s:v n21o:v a20:v f22:s a21:v f23:s p421o:v qz20:v a22:v r200:s r203:s r201:s r202:s p2s:v qz21:v a23:v r211:s r212:s r213:s qh20:v r210:s a24:v nxb:s sc20:g s20:s Snb:y qh21:v qz22:v ss20:g qv:v sc21:g p2o:v k202:s s21:v lo21:s lo20:v r220:s hi21:v r223:s r222:s r221:s hi20:v k203:s k201:s qh22:v k200:s b20:v sm20:v k211:s k210:v k213:s sg20:v sr20:s k212:v nr20:v k223:s nr21:v n30s:v pr20:v n30o:v k222:s nw2:g pr21:v n31s:v k220:s p430s:v k221:s p431s:v n31o:v p430o:v f31:v f30:s Sna:y p431o:v f32:s a30:v a31:v f33:s a32:v qz30:v qz31:v Sc0:y a33:v y0:s Sy0:y y1:s Sc1:y Sy1:y qz32:v Sc2:y Ss0:s y2:v Ss2:y Ss1:s Sy2:y Ss3:s
"""

SCRATCH = {"ps": ("psum", [128, 4096], F32)}
for _n, _w, _d in (("nxi", 44, I32), ("pri", 84, I32), ("nx16", 44, U16), ("n4", 112, U16), ("wq", 512, FP8), ("wsc", 512, U8),
                   ("ut", 512, BF16), ("uq0", 128, FP8), ("us0", 128, U8), ("uq", 128, FP8), ("us", 128, U8), ("uof", 8, U16),
                   ("vt", 512, BF16), ("vq", 128, FP8), ("vs", 128, U8), ("et", 128, BF16), ("eo", 516, BF16), ("eq", 512, FP8), ("es", 512, U8),
                   ("pci", 28, I32), ("qci", 32, I32), ("q16", 28, U16), ("col", 16, F32), ("nar", 240, F32),
                   ("d16", C, BF16), ("d4", C, BF16), ("uoi", 8, I32), ("i84", 84, F32),
                   ("iota", WC, F32), ("inv", WC, F32), ("nxr0", WC, F32), ("invh", C, F16), ("sigr", WC, F32),
                   ("sm", 252, F32), ("k3", 252, F32), ("scd", 9 * C + 32, F16), ("lohi", 168, F32), ("lh16", 168, U16),
                   ("sig", 84, U16), ("sb", 2 * C, F32), ("ysb", C, F32)):
    SCRATCH[_n] = ("sbuf", [128, _w], _d)
for _t in range(4):
    for _n, _w, _d in (("win", K, BF16), ("pb", 4 * C, BF16), ("z", 4 * C, BF16), ("zq", C, FP8), ("zs", C, U8), ("sh", 3 * C, F16), ("l", 252, U16)):
        SCRATCH[_n + str(_t)] = ("sbuf", [128, _w], _d)
for _t in range(3):
    for _n, _w, _d in (("h", 4 * C, BF16), ("hq", WC, FP8), ("hs", WC, U8), ("pvr", C, F16), ("ssb", C, F32), ("ssc", C, F32),
                       ("nxh", C, F16), ("cmp", C, BF16)):
        SCRATCH[_n + str(_t)] = ("sbuf", [128, _w], _d)
    SCRATCH["nxr%d" % (_t + 1)] = ("sbuf", [128, C], F32)

SEMAPHORES = ["cv", "cs", "cp", "cg", "sent", "st"] + ["ld%d" % i for i in range(8)] + ["arr%d" % t for t in range(3)]


def R(name, lo, hi, step=1):
    return (name, lo, hi, step)


def cuts(c):
    return list(zip(c[:-1], c[1:]))


def calls(g, core, T, topo, bank):
    rank = T.rank_of(core)
    A_, F_ = AluOpType, ActivationFunctionType
    V, S = g.vector, g.scalar
    dq = {"y": g.sync, "s": g.scalar}
    ops = []

    def op(name, qs, reads, writes, emit, sem=None):
        ops.append((name, qs, reads, writes, emit, sem))

    def ap(r):
        if r[0] == "@": return ap(r[1]).indirect(ap(r[2]))
        if r[0] == "ps": return T.ps[:, 512 * bank[r[1]]:512 * bank[r[1]] + r[2]]
        n, lo, hi, step = r
        return T[n][:, lo:hi] if step == 1 else T[n][:, lo:hi:step]

    def ind(win, off): return ("@", win, off)

    def flat(rs):
        o = []
        for r in rs:
            if isinstance(r, tuple): o += [r[1], r[2]] if r[0] == "@" else [r]
        return o

    def val(s): return ap(s) if isinstance(s, tuple) else s

    def tt(n, out, a, b, o): op(n, "v", flat([a, b]), [out], lambda q: V.tensor_tensor(ap(out), ap(a), ap(b), o))

    def tc(n, out, a): op(n, "v", flat([a]), [out], lambda q: V.tensor_copy(ap(out), ap(a)))

    def fill(n, out, c): op(n, "v", [], [out], lambda q: V.memset(ap(out), c))

    def ts(n, out, a, s1, s2, o0, o1=None):
        if o1 is None: op(n, "v", flat([a, s1]), [out], lambda q: V.tensor_scalar(ap(out), ap(a), val(s1), None, o0))
        else: op(n, "v", flat([a, s1, s2]), [out], lambda q: V.tensor_scalar(ap(out), ap(a), val(s1), val(s2), o0, o1))

    def scan(n, out, d0, d1, o0=A_.add, o1=A_.max):
        op(n, "v", [d0, d1], [out], lambda q: V.tensor_tensor_scan(ap(out), ap(d0), ap(d1), 0.0, o0, o1))

    def copy(n, qs, out, a):
        op(n, qs, flat([a]), [out], lambda q: S.activation(ap(out), ap(a), F_.Copy) if q == "s" else V.tensor_copy(ap(out), ap(a)))

    def affine(n, qs, out, a, mul, add):
        fn = F_.Identity if isinstance(add, tuple) else F_.Copy
        op(n, qs, flat([a, add]), [out], lambda q: S.activation(ap(out), ap(a), fn, bias=val(add), scale=mul) if q == "s"
           else V.tensor_scalar(ap(out), ap(a), mul, val(add), A_.mult, A_.add))

    def act(n, out, a, fn, mul, add):
        op(n, "s", flat([a, add]), [out], lambda q: S.activation(ap(out), ap(a), fn, bias=val(add), scale=mul))

    def relu(n, out, a):
        op(n, "sv", [a], [out], lambda q: S.activation(ap(out), ap(a), F_.Relu, scale=0.015625) if q == "s"
           else V.tensor_scalar(ap(out), ap(a), 0.0, 0.015625, A_.max, A_.mult))

    def quant(n, q, s, a, b, src):
        op(n, "v", [src], [R(q, a, b), R(s, a, b)], lambda _: V.quantize_mx(T[q][:, a:b], T[s][:, a:b], ap(src)))

    def mm(n, wq, ws, wa, xq, xs, a, b):
        o = ("ps", n, b - a, 1)
        op(n, "p", [R(wq, wa, wa + 128), R(ws, wa, wa + 128), R(xq, a, b), R(xs, a, b)], [o],
           lambda q: g.tensor.matmul_mx(ap(o), T[wq][:, wa:wa + 128], T[ws][:, wa:wa + 128], T[xq][:, a:b], T[xs][:, a:b], True, True))
        return o

    def iota(n, name, lo, hi, pattern, base, cm):
        o = R(name, lo, hi)
        if SCRATCH[name][2] == F32: op(n, "g", [], [o], lambda q: g.iota(ap(o), pattern, base, cm, allow_small_or_imprecise_dtypes=True))
        else: op(n, "g", [], [o], lambda q: g.iota(ap(o), pattern, base, cm))

    def gcopy(n, out, a):
        op(n, "g", [a], [out], lambda q: g.affine_select(ap(out), ap(a), [[0, a[2] - a[1]]], A_.is_ge, 0.0, 0, 0))

    nld = [0]

    def load(n, r, dst, src):
        op(n, "y", [], [r], lambda q: dq[q].dma_start(dst, src), "ld%d" % nld[0])
        nld[0] += 1

    def store(n, r, dst, src):
        op(n, "ys", [r], [], lambda q: dq[q].dma_start(dst, src), "st")

    load("Lnx", R("nxi", 0, 44), T.nxi[:], T.nx[:])
    load("Lx", R("win0", 0, 4 * C), T.win0[:, 0:4 * C], T.x[:])
    load("Lgh", R("win0", 4 * C, K), T.win0[:, 4 * C:K], T.gh[:])
    load("Lw", R("wq", 0, 512), T.wq[:, 0:512].bitcast(dt.uint8), T.wc[:])
    load("Lws", R("wsc", 0, 512), T.wsc[:], T.ws[:])
    load("Lu", R("ut", 0, 512), T.ut[:], T.u[:])
    load("Lpr", R("pri", 0, 84), T.pri[:], T.pr[:])
    load("Lv", R("vt", 0, 512), T.vt[:], T.v[:])

    col = lambda k: R("col", k, k + 1)
    Q, QH, QL, C16, CA, C4, C40 = [col(k) for k in range(7)]
    iota("Ip", "pci", 0, 28, [[0, 28]], 0, 1)
    iota("I16", "nar", 7, 32, [[1, 25]], -1, 0)
    iota("I4", "nar", 32, 48, [[0, 4], [1, 4]], 0, 0)
    iota("Ij", "iota", 0, WC // 4, [[1, WC // 4]], 0, 0)
    affine("i2", "sv", R("iota", WC // 4, WC // 2), R("iota", 0, WC // 4), 1.0, float(WC // 4))
    affine("i4", "sv", R("iota", WC // 2, WC), R("iota", 0, WC // 2), 1.0, float(WC // 2))
    iota("Iu", "uoi", 0, 8, [[16, 8]], 0, 0)
    iota("I84", "i84", 0, 84, [[0, 3], [16, 28]], 0, 0)
    fill("ones", R("et", 0, 128), 1.0)
    fill("zero", R("eo", 0, 516), 0.0)
    op("unit", "g", [R("et", 0, 128)], [R("eo", 3, 515, 4)],
       lambda q: g.affine_select(T.eo[:, 3:515:4], T.et[:], [[1, 128]], A_.is_equal, 0.0, 0, -1))
    for b in range(4): quant("qe%d" % b, "eq", "es", 128 * b, 128 * b + 128, R("eo", 3 - b, 515 - b))
    iota("Ig", "sigr", C, WC, [[1, G]], C, 0)
    affine("k0", "sv", R("k3", 0, 252, 3), R("iota", 0, 84), 0.0, 0.0)
    affine("k1", "sv", R("k3", 1, 252, 3), R("iota", 0, 84), 0.0, 1.0)
    ts("q", R("qci", 0, 28), R("pci", 0, 28), 15, None, A_.bitwise_and)
    ts("qh", R("qci", 28, 29), R("pci", 0, 1), 2, 3, A_.arith_shift_right, A_.bitwise_and)
    ts("ql", R("qci", 29, 30), R("pci", 0, 1), 3, None, A_.bitwise_and)
    tc("qf", R("col", 0, 3), R("qci", 27, 30))
    tc("q16", R("q16", 0, 28), R("qci", 0, 28))
    act("na", R("nar", 55, 80), R("nar", 7, 32), F_.Abs, -1.0, Q)
    act("nb", R("nar", 80, 96), R("nar", 32, 48), F_.Abs, -1.0, QH)
    act("nm", R("nar", 104, 145), R("nar", 55, 96), F_.Relu, -UP, UP)
    affine("nc", "sv", R("nar", 200, 240), R("nar", 105, 145), -4.0, 0.0)
    tt("nd", R("nar", 152, 192), R("nar", 200, 240), R("nar", 104, 144), A_.add)
    copy("d4", "s", R("d4", 0, C), ind(R("nar", 176, 192), R("q16", 0, 28)))
    copy("d16", "s", R("d16", 0, C), ind(R("nar", 152, 168), R("q16", 0, 28)))
    affine("c16", "sv", C16, R("nar", 120, 121), -1.0, UP)
    affine("ca", "sv", CA, R("nar", 132, 133), -1.0, UP)
    affine("c4", "sv", C4, QL, -float(WC), CA)
    affine("c40", "sv", C40, QL, -0.25, CA)
    PD, JW = R("k3", 2, 252, 3), R("scd", 77, 77 + 48 * 83 + 1, 48)
    ts("jw", JW, R("i84", 0, 84), Q, None, A_.add)
    ts("ul", R("scd", 61, 61 + 48 * 83 + 1, 48), R("i84", 0, 84), 0.0, C16, A_.mult, A_.subtract)

    def four(n, t, k, row, a, b):
        sb = "sh%d" % t if t else "sb"
        scan(n + "s", R(sb, C * k + a, C * k + b), R("d4", a, b), R(row, a, b))
        o, s = R("l%d" % t, 112 * k + a // 4, 112 * k + b // 4), R(sb, C * k + a + 3, C * k + b, 4)
        if t == 0: ts(n + "o", o, s, C40, 4.0, A_.subtract, A_.mult)
        else: ts(n + "o", o, s, C4, None, A_.subtract)

    def previous(t, row):
        for i, (a, b) in enumerate(cuts(CFG["pv"][t])): four("p4%d%d" % (t, i), t, 1, row, a, b)
        if t < ROUNDS:
            sb = "sh%d" % t
            scan("p%ds" % t, R(sb, 2 * C, 3 * C), R("d16", 0, C), R(row if t else "invh", 0, C))
            ts("p%do" % t, R("l%d" % t, 224, 252), R(sb, 2 * C + 15, 3 * C, 16), C16, None, A_.subtract)

    tc("nx16", R("nx16", 0, 44), R("nxi", 0, 44))
    for e in range(4): ts("n4%d" % e, R("n4", 28 * e, 28 * e + 28), R("nxi", 0, 28), 4.0, float(e), A_.mult, A_.add)
    op("inv", "v", [R("nx16", 0, 44), R("iota", 0, WC)], [R("inv", 0, WC)],
       lambda q: V.tensor_copy(T.inv[:, 0:WC].indirect(T.nx16[:, 0:44]), T.iota[:, 0:WC]))
    gcopy("ih", R("invh", 0, C), R("inv", 0, C))
    previous(0, "inv")
    copy("nxa", "sv", R("nxr0", 0, C), ind(R("iota", 0, WC), R("nx16", 0, 28)))
    copy("nxb", "sv", R("nxr0", C, WC), ind(R("iota", 0, WC), R("nx16", 28, 44)))
    store("Snb", R("nxr0", C, WC), T.nl[:, C:WC], T.nxr0[0:128:16, C:WC])
    tc("uof", R("uof", 0, 8), R("uoi", 0, 8))
    quant("qu", "uq0", "us0", 0, 128, R("ut", 0, 512))
    op("uq", "v", [R("uq0", 0, 128), R("uof", 0, 8)], [R("uq", 0, 128)],
       lambda q: V.tensor_copy(T.uq[:, 0:128].bitcast(dt.uint32), T.uq0[:, 0:128].bitcast(dt.uint32).indirect(T.uof[:, 0:8])))
    copy("us", "sv", R("us", 0, 128), ind(R("us0", 0, 128), R("uof", 0, 8)))
    quant("qv", "vq", "vs", 0, 128, R("vt", 0, 512))
    tt("lo", R("lohi", 0, 84), R("pri", 0, 84), JW, A_.min)
    tt("hi", R("lohi", 84, 168), R("pri", 0, 84), JW, A_.max)
    tc("lh", R("lh16", 0, 168), R("lohi", 0, 168))
    tt("pd", PD, R("pri", 0, 84), JW, A_.subtract)

    def reading(t):
        w, l, pb, z = R("win%d" % t, 0, K), "l%d" % t, "pb%d" % t, "z%d" % t
        for i, (a, b) in enumerate(cuts(CFG["f"][t])):
            n = "%d%d" % (t, i)
            if t == 0:
                for e in range(4): copy("f%s%d" % (n, e), "sv", R(pb, 4 * a + e, 4 * b, 4), ind(w, R("n4", 28 * e + a // 16, 28 * e + b // 16)))
            else: copy("f" + n, "sv", R(pb, 4 * a, 4 * b), ind(w, R(l, a // 4, b // 4)))
        for i, (a, b) in enumerate(cuts(CFG["a"][t])):
            tt("a%d%d" % (t, i), R(z, 4 * a, 4 * b), ind(w, R(l, 112 + a // 4, 112 + b // 4)), R(pb, 4 * a, 4 * b), A_.add)
        for i, (a, b) in enumerate(cuts(CFG["qz"][t])): quant("qz%d%d" % (t, i), "zq%d" % t, "zs%d" % t, a, b, R(z, 4 * a, 4 * b))

    def send(t):
        dst = T.cores[rank ^ (1 << t)]
        rid, pid, _ = topo.addr(dst)
        e, m, pieces = topo.engines(core, dst), topo.mask(core, dst), cuts(CFG["send"][t])
        h, s, arr = "hq%d" % t, "hs%d" % t, "arr%d" % t
        sem = (arr, len(e), len(e) * (len(pieces) + 1))
        for i, (a, b) in enumerate(pieces):
            op("sc%d%d" % (t, i), "g", [R(h, a, b)], [R(h, C + a, C + b)], lambda q, a=a, b=b: g.remote_dma(
                T[h][:, C + a:C + b].bitcast(dt.uint8), T[h][:, a:b].bitcast(dt.uint8), T.sem[arr], T.sem.sent, pid, rid, m), sem)
        op("ss%d0" % t, "g", [R(s, 0, G)], [R(s, C, WC)], lambda q: g.remote_dma(T[s][:, C:WC], T[s][:, 0:G], T.sem[arr], T.sem.sent, pid, rid, m), sem)

    for t in range(ROUNDS):
        zq, zs, h, hq, hs, win = "zq%d" % t, "zs%d" % t, "h%d" % t, "hq%d" % t, "hs%d" % t, "win%d" % (t + 1)
        ssb, ssc, cmp, pvr, nr, nh = "ssb%d" % t, "ssc%d" % t, "cmp%d" % t, "pvr%d" % t, "nxr%d" % (t + 1), "nxh%d" % t
        reading(t)
        for i, (a, b) in enumerate(cuts(CFG["r"][t])):
            for k in range(4): relu("r%d%d%d" % (t, i, k), R(h, 4 * a + k, 4 * b, 4), mm("mw%d%d%d" % (t, i, k), "wq", "wsc", 128 * k, zq, zs, a, b))
        for i, (a, b) in enumerate(cuts(CFG["qh"][t])): quant("qh%d%d" % (t, i), hq, hs, a, b, R(h, 4 * a, 4 * b))
        send(t)
        for i, (a, b) in enumerate(cuts(CFG["score"][t])): copy("s%d%d" % (t, i), "sv", R(ssb, a, b), mm("mu%d%d" % (t, i), "uq", "us", 0, zq, zs, a, b))
        for i, (a, b) in enumerate(cuts(CFG["pair"][t])):
            o = 28 * t + a // 16, 28 * t + b // 16
            copy("lo%d%d" % (t, i), "sv", R(ssc, a, b), ind(R(ssb, 0, C), R("lh16", *o)))
            tt("hi%d%d" % (t, i), R(cmp, a, b), ind(R(ssb, 0, C), R("lh16", 84 + o[0], 84 + o[1])), R(ssc, a, b), A_.is_gt)
        for i, (a, b) in enumerate(cuts(CFG["sign"][t])):
            a3, b3 = 3 * (C * t + a), 3 * (C * t + b)
            scan("b%d%d" % (t, i), R("scd", a3, b3 - 2, 3), R("d16", a, b), R(cmp, a, b))
        for i, (a, b) in enumerate(cuts(CFG["sig"][t])):
            a3, b3 = 3 * (C * t + a), 3 * (C * t + b)
            scan("sm%d%d" % (t, i), R("sm", a3 // 16, b3 // 16), R("k3", a3 // 16, b3 // 16), R("scd", a3 + 45, b3 + 30, 16), A_.mult, A_.add)
            tc("sg%d%d" % (t, i), R("sig", a3 // 48, b3 // 48), R("sm", a3 // 16 + 2, b3 // 16, 3))
        for i, (a, b) in enumerate(cuts(CFG["sr"][t])):
            copy("sr%d%d" % (t, i), "sv", R("sigr", a, b), ind(R("iota", 0, C), R("sig", 28 * t + a // 16, 28 * t + b // 16)))
        for i, (a, b) in enumerate(cuts(CFG["nx"][t])):
            copy("nr%d%d" % (t, i), "v", R(nh, a, b), ind(R("nxr%d" % t, 0, C), R("sig", 28 * t + a // 16, 28 * t + b // 16)))
            four("n%d%d" % (t + 1, i), t + 1, 0, nh, a, b)
        gcopy("nw%d" % t, R(nr, 0, C), R(nh, 0, C))
        for i, (a, b) in enumerate(cuts(CFG["pv"][t + 1])):
            copy("pr%d%d" % (t, i), "v", R(pvr, a, b), ind(R("sigr", 0, WC), R("l%d" % t, 224 + a // 16, 224 + b // 16)))
        previous(t + 1, pvr)
        for i, (a, b) in enumerate(cuts(CFG["own"][t])):
            for k in range(4): copy("k%d%d%d" % (t, i, k), "sv", R(win, WC * k + a, WC * k + b), mm("me%d%d%d" % (t, i, k), "eq", "es", 128 * k, hq, hs, a, b))
    store("Sna", R("nxr3", 0, C), T.nl[:, 0:C], T.nxr3[0:128:16, 0:C])
    reading(3)
    for i, (a, b) in enumerate(cuts(CFG["qz"][3])):
        store("Sc%d" % i, R("zq3", a, b), T.oc[:, 4 * a:4 * b], T.zq3[:, a:b].bitcast(dt.uint8))
        copy("y%d" % i, "sv", R("ysb", a, b), mm("mv%d" % i, "vq", "vs", 0, "zq3", "zs3", a, b))
        store("Sy%d" % i, R("ysb", a, b), T.y[:, a:b], T.ysb[:, a:b])
    for k in range(4): store("Ss%d" % k, R("zs3", 0, C), T.osc[4 * k:4 * k + 4, 0:C], T.zs3[32 * k:32 * k + 4, 0:C])
    return ops


def clash(a, lo, hi, step):
    if a[1] <= lo or hi <= a[0]: return False
    return (a[0] - lo) % math.gcd(a[2], step) == 0


def rank_program(g, core, T, topo):
    if T.rank_of(core) is None:
        return
    bank = {}
    ops = calls(g, core, T, topo, bank)
    by = {o[0]: o for o in ops}
    seq = []
    for w in ORDER.split():
        name, q = w.split(":")
        seq += [(by[r[1]], "p") for r in by[name][2] if r[0] == "ps"] + [(by[name], q)]
    assert len(seq) == len(ops) == len({o[0][0] for o in seq})
    eng = {"v": g.vector, "s": g.scalar, "p": g.tensor, "g": g, "y": g.sync}
    csem = {"v": "cv", "s": "cs", "p": "cp", "g": "cg"}
    issued, waited = {}, {}
    known = {q: {} for q in eng}
    snap = {}
    log = {}
    free = list(range(8))

    def region(r):
        return ("bank%d" % bank[r[1]], 0, 512, 1) if r[0] == "ps" else r

    for (name, qs, reads, writes, emit, sem), q in seq:
        for r in writes:
            if r[0] == "ps": bank[r[1]] = free.pop(0)
        for r in reads:
            if r[0] == "ps": free.append(bank[r[1]])
        remote = isinstance(sem, tuple)
        need = {}
        for rs, wr in ((reads, False), ([] if remote else writes, True)):
            for r in rs:
                n, lo, hi, step = region(r)
                for a in log.get(n, []):
                    if (wr or a[3]) and clash(a, lo, hi, step): need[a[4][0]] = max(need.get(a[4][0], 0), a[4][1])
        kn = known[q]
        todo = [(s, v) for s, v in need.items() if kn.get(s, 0) < v]
        for s, v in todo:
            if any(s2 != s and snap.get((s2, v2), {}).get(s, 0) >= v for s2, v2 in todo): continue
            eng[q].wait_ge(T.sem[s], v)
            waited[s] = max(waited.get(s, 0), v)
        for s, v in todo:
            for s2, v2 in snap.get((s, v), {}).items(): kn[s2] = max(kn.get(s2, 0), v2)
            kn[s] = max(kn.get(s, 0), v)
        ins = emit(q)
        if remote:
            issued["sent"] = issued.get("sent", 0) + sem[1]
            tok = (sem[0], sem[2])
            issued[sem[0]] = sem[2]
            reads = []
        else:
            s, inc = (sem, 16) if sem else (csem[q], 1)
            issued[s] = issued.get(s, 0) + inc
            ins.then_inc(T.sem[s], inc)
            tok = (s, issued[s])
            snap[tok] = dict(kn)
        for rs, wr in ((reads, False), (writes, True)):
            for r in rs:
                n, lo, hi, step = region(r)
                w = wr or n[:4] == "bank"
                l = log.setdefault(n, [])
                if w and step == 1: l[:] = [a for a in l if not (lo <= a[0] and a[1] <= hi)]
                l.append((lo, hi, step, w, tok))
    for s in sorted(issued):
        if waited.get(s, 0) < issued[s]: (g if s == "sent" else g.sync).wait_ge(T.sem[s], issued[s])
